import numpy as np
import ml_dtypes


def mxq(x, axis, fmt="e4m3"):
    dtype, down = {"e4m3": (ml_dtypes.float8_e4m3fn, 7), "e5m2": (ml_dtypes.float8_e5m2, 14)}[fmt]
    v = np.moveaxis(np.asarray(x, np.float32).astype(ml_dtypes.bfloat16).astype(np.float64), axis, -1)
    blocks = v.reshape(v.shape[:-1] + (-1, 32))
    amax = np.abs(blocks).max(-1, keepdims=True)
    byte = np.maximum(np.where(amax > 0, np.frexp(amax)[1] - 1 + 127, 0) - down, 1)
    scale = np.exp2(byte - 127.0)
    codes = (blocks / scale).astype(np.float32).astype(dtype).astype(np.float64)
    return np.moveaxis((codes * scale).reshape(v.shape), -1, axis)


WIDE = False


def mx_kscale(k):
    if not WIDE:
        return np.ones(k)
    levels = np.array([10, -10, 5, -5, 0])
    if k % 512:
        return np.exp2(np.random.permutation(np.resize(levels, k // 32))).repeat(32)
    a = np.empty((k // 512, 16))
    for p in range(k // 512):
        a[p, :8] = np.random.permutation(np.resize(levels, 8))
        for g in range(8):
            far = levels[np.abs(levels - a[p, g]) >= 10]
            a[p, g + 8] = far[np.random.randint(len(far))]
    return np.exp2(a.ravel()).repeat(32)


def f64(x):
    return np.asarray(x).astype(np.float64)


def striped(idx):
    return np.tile(idx.reshape(-1, 16).T, (8, 1)).astype(np.uint16)


def unstriped(offs):
    return offs[:16].T.reshape(-1).astype(np.int64)


E2M1 = np.array([0.0, 0.5, 1.0, 1.5, 2.0, 3.0, 4.0, 6.0, -0.0, -0.5, -1.0, -1.5, -2.0, -3.0, -4.0, -6.0])


def pack_weight(w, fmt):
    k, n = w.shape
    w = f64(np.asarray(w, np.float32).astype(ml_dtypes.bfloat16)).reshape(k // 32, 32, n)
    amax = np.abs(w).max(1)
    if fmt == "e4m3":
        byte = np.frexp(amax)[1] - 1 + 127 - 7
    else:
        mant, ex = np.frexp(amax / 6.0)
        byte = np.where(mant > 0.5, ex, ex - 1) + 127
    byte = np.clip(np.where(amax > 0, byte, 1), 1, 254)
    scaled = (w * np.exp2(127.0 - byte)[:, None, :]).reshape(k, n).astype(np.float32)
    by_word = np.ascontiguousarray(scaled.reshape(k // 512, 128, 4, n).transpose(0, 1, 3, 2))
    if fmt == "e4m3":
        words = by_word.astype(ml_dtypes.float8_e4m3fn).view(np.uint8)
    else:
        c = by_word.astype(ml_dtypes.float4_e2m1fn).view(np.uint8) & 0xF
        words = (c[..., 0::2] | (c[..., 1::2] << 4)).reshape(k // 512, 128, 2 * n)
    return np.ascontiguousarray(words), np.ascontiguousarray(byte.astype(np.uint8).reshape(k // 512, 16, n))


def unpack_weight(words, scales, fmt):
    g, _, n = scales.shape
    words = np.ascontiguousarray(words).reshape(g, 128, n, -1)
    if fmt == "e4m3":
        vals = words.view(ml_dtypes.float8_e4m3fn).astype(np.float64)
    else:
        nib = np.empty((g, 128, n, 4), np.uint8)
        nib[..., 0::2] = words & 0xF
        nib[..., 1::2] = words >> 4
        vals = E2M1[nib]
    vals = vals * np.repeat(np.exp2(scales.astype(np.float64) - 127.0), 8, axis=1)[..., None]
    return vals.transpose(0, 1, 3, 2).reshape(g * 512, n)


K, M, T, S = 1536, 1024, 4096, 1536


def setup_inputs():
    n = np.random.standard_normal
    s = mx_kscale(K)[:, None]
    u = mx_kscale(512)[:, None]
    v = pack_weight(n((K, T)) * s, "e4m3")
    p_w4 = pack_weight(n((K, M)) / np.sqrt(K) / s, "e2m1")
    return {
        "tab_words": v[0],
        "tab_scales": v[1],
        "w4_words": p_w4[0],
        "w4_scales": p_w4[1],
        "down": (n((K, 512)) / np.sqrt(K) / s * u.T).astype(np.float32),
        "up": (0.5 * n((512, M)) / np.sqrt(512) / u).astype(np.float32),
        "gT": n((M, T)).astype(np.float32),
        "offs": striped(np.random.permutation(T)[:S]),
    }


def reference(tab_words, tab_scales, w4_words, w4_scales, down, up, gT, offs):
    tab_ = unpack_weight(tab_words, tab_scales, "e4m3")[:, unstriped(offs)]
    w4_ = unpack_weight(w4_words, w4_scales, "e2m1")
    down_ = mxq(f64(down), 0, "e4m3")
    up_ = mxq(f64(up), 0, "e4m3")
    h_ = mxq(down_.T @ tab_, 0, "e4m3")
    y = w4_.T @ tab_ + up_.T @ h_
    return (y) * f64(gT)[:, unstriped(offs)]

@@ -1,0 +1,204 @@
+from contextlib import ExitStack
+
+import concourse.mybir as mybir
+
+K, M, T, S, R = 1536, 1024, 4096, 1536, 512
+FLOPS = 2 * S * (K * R + K * M + R * M)
+
+F32 = mybir.dt.float32
+BF16 = mybir.dt.bfloat16
+I32 = mybir.dt.int32
+U32 = mybir.dt.uint32
+U16 = mybir.dt.uint16
+U8 = mybir.dt.uint8
+FP8X4 = mybir.dt.float8_e4m3fn_x4
+FP4X4 = mybir.dt.float4_e2m1fn_x4
+MULT = mybir.AluOpType.mult
+
+P = 128
+PACK = 4
+PASSES = K // (P * PACK)
+CHUNK = 512
+CHUNKS = S // CHUNK
+H_COLS = 128
+M_TILES = M // P
+LIST_COLS = CHUNK // 16
+
+SLOT_A, SLOT_B, SLOT_C, SLOT_D, SLOT_E, SLOT_F = 0, 16, 32, 48, 64, 80
+SLOT_W4 = 96
+STAGE = 105
+GATE_SLOTS = (SLOT_D, SLOT_A, SLOT_B, SLOT_C, SLOT_E, SLOT_F, SLOT_D, SLOT_A)
+
+
+def tile_list_tabgate_none_kernel(
+    tc, tab_words, tab_scales, w4_words, w4_scales, down, up, gT, offs, out
+):
+    nc = tc.nc
+    with ExitStack() as ctx:
+        keep = ctx.enter_context(tc.tile_pool(name="keep", bufs=1))
+        arena = ctx.enter_context(tc.tile_pool(name="arena", bufs=1))
+        ring = ctx.enter_context(tc.tile_pool(name="ring", bufs=3))
+        psum_h = ctx.enter_context(tc.psum_pool(name="psum_h", bufs=3))
+        psum_y = ctx.enter_context(tc.psum_pool(name="psum_y", bufs=5))
+
+        def placed(shape, dtype, name, kib):
+            return arena.tile(shape, dtype, name=name, offset=1024 * kib, align_bytes=64)
+
+        offsets = keep.tile([P, S // 16], U16, name="offsets")
+        nc.sync.dma_start(offsets[:], offs)
+
+        scale_rows = tab_scales.bitcast(I32).rearrange("a q t -> (a q) t")
+        scale_window = placed([P, T // 4], I32, "scale_window", SLOT_A)
+        for first_partition, count, first_row in ((0, 16, 0), (16, 16, 32), (32, 32, 4), (64, 32, 8), (96, 32, 12)):
+            nc.sync.dma_start(
+                out=scale_window[first_partition : first_partition + count, :],
+                in_=scale_rows[first_row : first_row + count, :],
+            )
+        down_raw = []
+        for a, kib in enumerate((SLOT_B, SLOT_C, SLOT_W4)):
+            raw = placed([P, PACK, R], F32, "down_raw%d" % a, kib)
+            nc.sync.dma_start(out=raw[:], in_=down[512 * a : 512 * (a + 1), :].rearrange("(p j) r -> p j r", j=PACK))
+            down_raw.append(raw)
+
+        tab_raw = []
+
+        def load_words(a, kib):
+            words = placed([P, T], I32, "tab_raw%d" % a, kib)
+            nc.sync.dma_start(out=words[:], in_=tab_words[a].rearrange("p t i -> p (t i)").bitcast(I32))
+            tab_raw.append(words)
+
+        load_words(0, SLOT_D)
+
+        picked_scales = keep.tile([P, S], U8, name="picked_scales", align_bytes=64)
+        moved_scales = keep.tile([P, PASSES - 1, S // 4], I32, name="moved_scales", align_bytes=64)
+        nc.vector.memset(moved_scales[:], 0)
+        nc.vector.tensor_copy(picked_scales[:], scale_window[:].bitcast(U8).indirect(offsets[:]))
+
+        def move_scales(a, first_partition):
+            for q in range(4):
+                nc.sync.dma_start(
+                    out=moved_scales[32 * q : 32 * q + 4, a - 1, :],
+                    in_=picked_scales[first_partition + 4 * q : first_partition + 4 * q + 4, :].bitcast(I32),
+                )
+
+        move_scales(1, 44)
+        load_words(1, SLOT_A)
+        move_scales(2, 16)
+        v_plane = [picked_scales[:], moved_scales[:, 0, :].bitcast(U8), moved_scales[:, 1, :].bitcast(U8)]
+
+        down_codes = keep.tile([P, PASSES, R], U32, name="down_codes", align_bytes=64)
+        down_plane = keep.tile([P, PASSES, R], U8, name="down_plane", align_bytes=64)
+        for a in range(PASSES):
+            grouped = placed([P, R * PACK], BF16, "down_grouped%d" % a, STAGE + 4 * a)
+            nc.scalar.copy(
+                out=grouped[:].rearrange("p (t m j) -> p m j t", t=PACK, j=PACK),
+                in_=down_raw[a][:].rearrange("p j (m t) -> p m j t", t=PACK),
+            )
+            nc.vector.quantize_mx(
+                out=down_codes[:, a, :].bitcast(FP8X4), scales=down_plane[:, a, :], in_=grouped[:]
+            )
+
+        load_words(2, SLOT_B)
+        up_raw = placed([P, PACK, M], F32, "up_raw", SLOT_C)
+        nc.sync.dma_start(out=up_raw[:], in_=up.rearrange("(p j) n -> p j n", j=PACK))
+        w4_codes = placed([P, PASSES, 2 * M], U8, "w4_codes", SLOT_W4)
+        nc.sync.dma_start(
+            out=w4_codes[:].bitcast(I32), in_=w4_words.bitcast(I32).rearrange("a p b -> p a b")
+        )
+        w4_plane = placed([P, PASSES, M // 4], I32, "w4_plane", SLOT_W4 + 6)
+        nc.vector.memset(w4_plane[:], 0)
+        for q in range(4):
+            nc.sync.dma_start(
+                out=w4_plane[32 * q : 32 * q + 4, :, :],
+                in_=w4_scales.bitcast(I32)[:, 4 * q : 4 * q + 4, :].rearrange("a r t -> r a t"),
+            )
+
+        v_codes = keep.tile([P, PASSES, S], U32, name="v_codes", align_bytes=64)
+        for a in range(PASSES - 1):
+            nc.vector.tensor_copy(v_codes[:, a, :], tab_raw[a][:].bitcast(U32).indirect(offsets[:]))
+        a = PASSES - 1
+        for c in range(CHUNKS):
+            nc.vector.tensor_copy(
+                v_codes[:, a, CHUNK * c : CHUNK * (c + 1)],
+                tab_raw[a][:].bitcast(U32).indirect(offsets[:, LIST_COLS * c : LIST_COLS * (c + 1)]),
+            )
+
+        up_codes = keep.tile([P, M], U32, name="up_codes", align_bytes=64)
+        up_plane = keep.tile([P, M], U8, name="up_plane", align_bytes=64)
+        for half in range(2):
+            cols = slice(512 * half, 512 * (half + 1))
+            grouped = placed([P, 512 * PACK], BF16, "up_grouped%d" % half, (STAGE, SLOT_E)[half])
+            nc.vector.tensor_copy(
+                out=grouped[:].rearrange("p (c i j) -> p c j i", i=4, j=PACK),
+                in_=up_raw[:, :, cols].rearrange("p j (c i) -> p c j i", i=4),
+            )
+            nc.vector.quantize_mx(out=up_codes[:, cols].bitcast(FP8X4), scales=up_plane[:, cols], in_=grouped[:])
+
+        h_codes = keep.tile([P, S], U32, name="h_codes", align_bytes=64)
+        h_plane = keep.tile([P, S], U8, name="h_plane", align_bytes=64)
+        for c in range(CHUNKS):
+            grouped = placed([P, CHUNK * PACK], BF16, "h_grouped%d" % c, (STAGE + 4, STAGE + 8, SLOT_F)[c])
+            for b in range(CHUNK // H_COLS):
+                cols = slice(CHUNK * c + H_COLS * b, CHUNK * c + H_COLS * (b + 1))
+                bank = psum_h.tile([P, PACK, H_COLS], F32, name="h_bank")
+                for t in range(PACK):
+                    for a in range(PASSES):
+                        nc.tensor.matmul_mx(
+                            out=bank[:, t, :],
+                            lhsT=down_codes[:, a, P * t : P * (t + 1)].bitcast(FP8X4),
+                            lhsT_scale=down_plane[:, a, P * t : P * (t + 1)],
+                            rhs=v_codes[:, a, cols].bitcast(FP8X4),
+                            rhs_scale=v_plane[a][:, cols],
+                            start=(a == 0),
+                            stop=(a == PASSES - 1),
+                        )
+                nc.scalar.copy(
+                    out=grouped[:, H_COLS * PACK * b : H_COLS * PACK * (b + 1)].rearrange("p (n t) -> p n t", t=PACK),
+                    in_=bank[:].rearrange("p t n -> p n t"),
+                )
+            cols = slice(CHUNK * c, CHUNK * (c + 1))
+            nc.vector.quantize_mx(out=h_codes[:, cols].bitcast(FP8X4), scales=h_plane[:, cols], in_=grouped[:])
+
+        gates = []
+        for m in range(M_TILES):
+            gate_rows = placed([P, T], F32, "gates%d" % m, GATE_SLOTS[m])
+            nc.sync.dma_start(out=gate_rows[:], in_=gT[P * m : P * (m + 1), :])
+            gates.append(gate_rows)
+
+        result = keep.tile([P, M_TILES, S], F32, name="result")
+        for m in range(M_TILES):
+            rows = slice(P * m, P * (m + 1))
+            y_sb = ring.tile([P, S], F32, name="y_sb", tag="y_sb")
+            for c in range(CHUNKS):
+                cols = slice(CHUNK * c, CHUNK * (c + 1))
+                acc = psum_y.tile([P, CHUNK], F32, name="y_bank")
+                for a in range(PASSES):
+                    nc.tensor.matmul_mx(
+                        out=acc[:],
+                        lhsT=w4_codes[:, a, 2 * P * m : 2 * P * (m + 1)].bitcast(FP4X4),
+                        lhsT_scale=w4_plane[:, a, :].bitcast(U8)[:, rows],
+                        rhs=v_codes[:, a, cols].bitcast(FP8X4),
+                        rhs_scale=v_plane[a][:, cols],
+                        start=(a == 0),
+                        stop=False,
+                    )
+                nc.tensor.matmul_mx(
+                    out=acc[:],
+                    lhsT=up_codes[:, rows].bitcast(FP8X4),
+                    lhsT_scale=up_plane[:, rows],
+                    rhs=h_codes[:, cols].bitcast(FP8X4),
+                    rhs_scale=h_plane[:, cols],
+                    start=False,
+                    stop=True,
+                )
+                nc.scalar.copy(out=y_sb[:, cols], in_=acc[:])
+                nc.vector.tensor_tensor(
+                    result[:, m, cols],
+                    gates[m][:].indirect(offsets[:, LIST_COLS * c : LIST_COLS * (c + 1)]),
+                    y_sb[:, cols],
+                    MULT,
+                )
+                if m == M_TILES - 1:
+                    nc.sync.dma_start(out=out[rows, cols], in_=result[:, m, cols])
+            if m < M_TILES - 1:
+                nc.sync.dma_start(out=out[rows, :], in_=result[:, m, :])

@@ -24,8 +24,8 @@ H_COLS = 128
 M_TILES = M // P
 LIST_COLS = CHUNK // 16
 
-SLOT_A, SLOT_B, SLOT_C, SLOT_D, SLOT_E, SLOT_F = 0, 16, 32, 48, 64, 80
-SLOT_W4 = 96
+SLOT_A, SLOT_B, SLOT_C, SLOT_D, SLOT_E, SLOT_F = 0, 16, 32, 57, 73, 89
+SLOT_W4 = 48
 STAGE = 105
 GATE_SLOTS = (SLOT_D, SLOT_A, SLOT_B, SLOT_C, SLOT_E, SLOT_F, SLOT_D, SLOT_A)
 
@@ -48,14 +48,12 @@ def tile_list_tabgate_none_kernel(
         nc.sync.dma_start(offsets[:], offs)
 
         scale_rows = tab_scales.bitcast(I32).rearrange("a q t -> (a q) t")
-        scale_window = placed([P, T // 4], I32, "scale_window", SLOT_A)
-        for first_partition, count, first_row in ((0, 16, 0), (16, 16, 32), (32, 32, 4), (64, 32, 8), (96, 32, 12)):
-            nc.sync.dma_start(
-                out=scale_window[first_partition : first_partition + count, :],
-                in_=scale_rows[first_row : first_row + count, :],
-            )
+        scale_window = placed([P, T // 4], I32, "scale_window", SLOT_B - 2)
+        nc.vector.memset(scale_window[:], 0)
+        nc.scalar.dma_start(out=scale_window[0:P:4, :], in_=scale_rows[0:32, :])
+        nc.scalar.dma_start(out=scale_window[1:P:8, :], in_=scale_rows[32:48, :])
         down_raw = []
-        for a, kib in enumerate((SLOT_B, SLOT_C, SLOT_W4)):
+        for a, kib in enumerate((SLOT_E, SLOT_F, SLOT_W4 - 4)):
             raw = placed([P, PACK, R], F32, "down_raw%d" % a, kib)
             nc.sync.dma_start(out=raw[:], in_=down[512 * a : 512 * (a + 1), :].rearrange("(p j) r -> p j r", j=PACK))
             down_raw.append(raw)
@@ -70,21 +68,24 @@ def tile_list_tabgate_none_kernel(
         load_words(0, SLOT_D)
 
         picked_scales = keep.tile([P, S], U8, name="picked_scales", align_bytes=64)
-        moved_scales = keep.tile([P, PASSES - 1, S // 4], I32, name="moved_scales", align_bytes=64)
+        moved_scales = keep.tile([P, PASSES, S // 4], I32, name="moved_scales", align_bytes=64)
         nc.vector.memset(moved_scales[:], 0)
         nc.vector.tensor_copy(picked_scales[:], scale_window[:].bitcast(U8).indirect(offsets[:]))
 
-        def move_scales(a, first_partition):
-            for q in range(4):
+        def move_scales(a, first_partition, step):
+            for r in range(4):
+                start = first_partition + step * r
                 nc.sync.dma_start(
-                    out=moved_scales[32 * q : 32 * q + 4, a - 1, :],
-                    in_=picked_scales[first_partition + 4 * q : first_partition + 4 * q + 4, :].bitcast(I32),
+                    out=moved_scales[r:P:32, a, :],
+                    in_=picked_scales[start : start + 12 * step + 1 : 4 * step, :].bitcast(I32),
                 )
 
-        move_scales(1, 44)
+        move_scales(0, 0, 4)
         load_words(1, SLOT_A)
-        move_scales(2, 16)
-        v_plane = [picked_scales[:], moved_scales[:, 0, :].bitcast(U8), moved_scales[:, 1, :].bitcast(U8)]
+        move_scales(1, 64, 4)
+        load_words(2, SLOT_B)
+        move_scales(2, 1, 8)
+        v_plane = [moved_scales[:, a, :].bitcast(U8) for a in range(PASSES)]
 
         down_codes = keep.tile([P, PASSES, R], U32, name="down_codes", align_bytes=64)
         down_plane = keep.tile([P, PASSES, R], U8, name="down_plane", align_bytes=64)
@@ -98,19 +99,18 @@ def tile_list_tabgate_none_kernel(
                 out=down_codes[:, a, :].bitcast(FP8X4), scales=down_plane[:, a, :], in_=grouped[:]
             )
 
-        load_words(2, SLOT_B)
         up_raw = placed([P, PACK, M], F32, "up_raw", SLOT_C)
         nc.sync.dma_start(out=up_raw[:], in_=up.rearrange("(p j) n -> p j n", j=PACK))
-        w4_codes = placed([P, PASSES, 2 * M], U8, "w4_codes", SLOT_W4)
+        w4_codes = placed([P, PASSES, 2 * M], U8, "w4_codes", SLOT_W4 + 3)
         nc.sync.dma_start(
             out=w4_codes[:].bitcast(I32), in_=w4_words.bitcast(I32).rearrange("a p b -> p a b")
         )
-        w4_plane = placed([P, PASSES, M // 4], I32, "w4_plane", SLOT_W4 + 6)
+        w4_plane = placed([P, PASSES, M // 4], I32, "w4_plane", SLOT_W4)
         nc.vector.memset(w4_plane[:], 0)
-        for q in range(4):
+        for r in range(4):
             nc.sync.dma_start(
-                out=w4_plane[32 * q : 32 * q + 4, :, :],
-                in_=w4_scales.bitcast(I32)[:, 4 * q : 4 * q + 4, :].rearrange("a r t -> r a t"),
+                out=w4_plane[r:P:32, :, :],
+                in_=w4_scales.bitcast(I32)[:, r:16:4, :].rearrange("a q t -> q a t"),
             )
 
         v_codes = keep.tile([P, PASSES, S], U32, name="v_codes", align_bytes=64)

@@ -27,6 +27,7 @@ LIST_COLS = CHUNK // 16
 SLOT_A, SLOT_B, SLOT_C, SLOT_D, SLOT_E, SLOT_F = 0, 16, 32, 57, 73, 89
 SLOT_W4 = 48
 STAGE = 105
+STORE_FROM = {2: 0, 5: 3, 6: 6, 7: 7}
 GATE_SLOTS = (SLOT_D, SLOT_A, SLOT_B, SLOT_C, SLOT_E, SLOT_F, SLOT_D, SLOT_A)
 
 
@@ -52,11 +53,12 @@ def tile_list_tabgate_none_kernel(
         nc.vector.memset(scale_window[:], 0)
         nc.scalar.dma_start(out=scale_window[0:P:4, :], in_=scale_rows[0:32, :])
         nc.scalar.dma_start(out=scale_window[1:P:8, :], in_=scale_rows[32:48, :])
-        down_raw = []
-        for a, kib in enumerate((SLOT_E, SLOT_F, SLOT_W4 - 4)):
-            raw = placed([P, PACK, R], F32, "down_raw%d" % a, kib)
-            nc.sync.dma_start(out=raw[:], in_=down[512 * a : 512 * (a + 1), :].rearrange("(p j) r -> p j r", j=PACK))
-            down_raw.append(raw)
+        down_rows = down.rearrange("(a p j) r -> p a j r", p=P, j=PACK)
+        down_early = placed([P, 2, PACK, R], F32, "down_early", SLOT_E)
+        nc.sync.dma_start(out=down_early[:], in_=down_rows[:, 0:2, :, :])
+        down_last = placed([P, PACK, R], F32, "down_last", SLOT_W4 - 4)
+        nc.sync.dma_start(out=down_last[:], in_=down_rows[:, 2, :, :])
+        down_raw = [down_early[:, 0, :, :], down_early[:, 1, :, :], down_last[:]]
 
         tab_raw = []
 
@@ -93,7 +95,7 @@ def tile_list_tabgate_none_kernel(
             grouped = placed([P, R * PACK], BF16, "down_grouped%d" % a, STAGE + 4 * a)
             nc.scalar.copy(
                 out=grouped[:].rearrange("p (t m j) -> p m j t", t=PACK, j=PACK),
-                in_=down_raw[a][:].rearrange("p j (m t) -> p m j t", t=PACK),
+                in_=down_raw[a].rearrange("p j (m t) -> p m j t", t=PACK),
             )
             nc.vector.quantize_mx(
                 out=down_codes[:, a, :].bitcast(FP8X4), scales=down_plane[:, a, :], in_=grouped[:]
@@ -136,7 +138,8 @@ def tile_list_tabgate_none_kernel(
 
         h_codes = keep.tile([P, S], U32, name="h_codes", align_bytes=64)
         h_plane = keep.tile([P, S], U8, name="h_plane", align_bytes=64)
-        for c in range(CHUNKS):
+
+        def make_h(c):
             grouped = placed([P, CHUNK * PACK], BF16, "h_grouped%d" % c, (STAGE + 4, STAGE + 8, SLOT_F)[c])
             for b in range(CHUNK // H_COLS):
                 cols = slice(CHUNK * c + H_COLS * b, CHUNK * c + H_COLS * (b + 1))
@@ -160,45 +163,61 @@ def tile_list_tabgate_none_kernel(
             nc.vector.quantize_mx(out=h_codes[:, cols].bitcast(FP8X4), scales=h_plane[:, cols], in_=grouped[:])
 
         gates = []
-        for m in range(M_TILES):
+
+        def load_gates(m):
             gate_rows = placed([P, T], F32, "gates%d" % m, GATE_SLOTS[m])
             nc.sync.dma_start(out=gate_rows[:], in_=gT[P * m : P * (m + 1), :])
             gates.append(gate_rows)
 
         result = keep.tile([P, M_TILES, S], F32, name="result")
-        for m in range(M_TILES):
+        y_tiles = []
+
+        def make_out(m, c):
             rows = slice(P * m, P * (m + 1))
-            y_sb = ring.tile([P, S], F32, name="y_sb", tag="y_sb")
-            for c in range(CHUNKS):
-                cols = slice(CHUNK * c, CHUNK * (c + 1))
-                acc = psum_y.tile([P, CHUNK], F32, name="y_bank")
-                for a in range(PASSES):
-                    nc.tensor.matmul_mx(
-                        out=acc[:],
-                        lhsT=w4_codes[:, a, 2 * P * m : 2 * P * (m + 1)].bitcast(FP4X4),
-                        lhsT_scale=w4_plane[:, a, :].bitcast(U8)[:, rows],
-                        rhs=v_codes[:, a, cols].bitcast(FP8X4),
-                        rhs_scale=v_plane[a][:, cols],
-                        start=(a == 0),
-                        stop=False,
-                    )
+            cols = slice(CHUNK * c, CHUNK * (c + 1))
+            if c == 0:
+                y_tiles.append(ring.tile([P, S], F32, name="y_sb", tag="y_sb"))
+            acc = psum_y.tile([P, CHUNK], F32, name="y_bank")
+            for a in range(PASSES):
                 nc.tensor.matmul_mx(
                     out=acc[:],
-                    lhsT=up_codes[:, rows].bitcast(FP8X4),
-                    lhsT_scale=up_plane[:, rows],
-                    rhs=h_codes[:, cols].bitcast(FP8X4),
-                    rhs_scale=h_plane[:, cols],
-                    start=False,
-                    stop=True,
+                    lhsT=w4_codes[:, a, 2 * P * m : 2 * P * (m + 1)].bitcast(FP4X4),
+                    lhsT_scale=w4_plane[:, a, :].bitcast(U8)[:, rows],
+                    rhs=v_codes[:, a, cols].bitcast(FP8X4),
+                    rhs_scale=v_plane[a][:, cols],
+                    start=(a == 0),
+                    stop=False,
                 )
-                nc.scalar.copy(out=y_sb[:, cols], in_=acc[:])
-                nc.vector.tensor_tensor(
-                    result[:, m, cols],
-                    gates[m][:].indirect(offsets[:, LIST_COLS * c : LIST_COLS * (c + 1)]),
-                    y_sb[:, cols],
-                    MULT,
-                )
-                if m == M_TILES - 1:
-                    nc.sync.dma_start(out=out[rows, cols], in_=result[:, m, cols])
-            if m < M_TILES - 1:
-                nc.sync.dma_start(out=out[rows, :], in_=result[:, m, :])
+            nc.tensor.matmul_mx(
+                out=acc[:],
+                lhsT=up_codes[:, rows].bitcast(FP8X4),
+                lhsT_scale=up_plane[:, rows],
+                rhs=h_codes[:, cols].bitcast(FP8X4),
+                rhs_scale=h_plane[:, cols],
+                start=False,
+                stop=True,
+            )
+            nc.scalar.copy(out=y_tiles[m][:, cols], in_=acc[:])
+            nc.vector.tensor_tensor(
+                result[:, m, cols],
+                gates[m][:].indirect(offsets[:, LIST_COLS * c : LIST_COLS * (c + 1)]),
+                y_tiles[m][:, cols],
+                MULT,
+            )
+
+        out_rows = out.rearrange("(m p) s -> p m s", p=P)
+        for m in range(5):
+            load_gates(m)
+        make_h(0)
+        make_h(1)
+        make_out(0, 0)
+        make_out(0, 1)
+        make_h(2)
+        for m in range(5, M_TILES):
+            load_gates(m)
+        make_out(0, 2)
+        for m in range(1, M_TILES):
+            for c in range(CHUNKS):
+                make_out(m, c)
+            if m in STORE_FROM:
+                nc.sync.dma_start(out=out_rows[:, STORE_FROM[m] : m + 1, :], in_=result[:, STORE_FROM[m] : m + 1, :])

@@ -28,7 +28,7 @@ SLOT_A, SLOT_B, SLOT_C, SLOT_D, SLOT_E, SLOT_F = 0, 16, 32, 57, 73, 89
 SLOT_W4 = 48
 STAGE = 105
 STORE_FROM = {2: 0, 5: 3, 6: 6, 7: 7}
-GATE_SLOTS = (SLOT_D, SLOT_A, SLOT_B, SLOT_C, SLOT_E, SLOT_F, SLOT_D, SLOT_A)
+GATE_SLOTS = (SLOT_B, SLOT_D, SLOT_C, SLOT_A, SLOT_E, SLOT_F, SLOT_B, SLOT_D)
 
 
 def tile_list_tabgate_none_kernel(
@@ -166,7 +166,7 @@ def tile_list_tabgate_none_kernel(
 
         def load_gates(m):
             gate_rows = placed([P, T], F32, "gates%d" % m, GATE_SLOTS[m])
-            nc.sync.dma_start(out=gate_rows[:], in_=gT[P * m : P * (m + 1), :])
+            (nc.scalar, nc.sync)[m % 2].dma_start(out=gate_rows[:], in_=gT[P * m : P * (m + 1), :])
             gates.append(gate_rows)
 
         result = keep.tile([P, M_TILES, S], F32, name="result")
@@ -220,4 +220,4 @@ def tile_list_tabgate_none_kernel(
             for c in range(CHUNKS):
                 make_out(m, c)
             if m in STORE_FROM:
-                nc.sync.dma_start(out=out_rows[:, STORE_FROM[m] : m + 1, :], in_=result[:, STORE_FROM[m] : m + 1, :])
+                (nc.scalar, nc.sync)[m % 2].dma_start(out=out_rows[:, STORE_FROM[m] : m + 1, :], in_=result[:, STORE_FROM[m] : m + 1, :])

@@ -24,11 +24,11 @@ H_COLS = 128
 M_TILES = M // P
 LIST_COLS = CHUNK // 16
 
-SLOT_A, SLOT_B, SLOT_C, SLOT_D, SLOT_E, SLOT_F = 0, 16, 32, 57, 73, 89
-SLOT_W4 = 48
-STAGE = 105
-STORE_FROM = {2: 0, 5: 3, 6: 6, 7: 7}
-GATE_SLOTS = (SLOT_B, SLOT_D, SLOT_C, SLOT_A, SLOT_E, SLOT_F, SLOT_B, SLOT_D)
+SLOT = 16
+SPARE = SLOT * M_TILES
+V_BYTES = PASSES * S
+W4_BYTES = PASSES * M
+STORE_GROUPS = ((0, 3, SPARE), (3, 6, 0), (6, 7, 18), (7, 8, 24))
 
 
 def tile_list_tabgate_none_kernel(
@@ -38,86 +38,74 @@ def tile_list_tabgate_none_kernel(
     with ExitStack() as ctx:
         keep = ctx.enter_context(tc.tile_pool(name="keep", bufs=1))
         arena = ctx.enter_context(tc.tile_pool(name="arena", bufs=1))
-        ring = ctx.enter_context(tc.tile_pool(name="ring", bufs=3))
+        ring = ctx.enter_context(tc.tile_pool(name="ring", bufs=4))
         psum_h = ctx.enter_context(tc.psum_pool(name="psum_h", bufs=3))
         psum_y = ctx.enter_context(tc.psum_pool(name="psum_y", bufs=5))
 
         def placed(shape, dtype, name, kib):
             return arena.tile(shape, dtype, name=name, offset=1024 * kib, align_bytes=64)
 
-        offsets = keep.tile([P, S // 16], U16, name="offsets")
-        nc.sync.dma_start(offsets[:], offs)
-
-        scale_rows = tab_scales.bitcast(I32).rearrange("a q t -> (a q) t")
-        scale_window = placed([P, T // 4], I32, "scale_window", SLOT_B - 2)
-        nc.vector.memset(scale_window[:], 0)
-        nc.scalar.dma_start(out=scale_window[0:P:4, :], in_=scale_rows[0:32, :])
-        nc.scalar.dma_start(out=scale_window[1:P:8, :], in_=scale_rows[32:48, :])
-        down_rows = down.rearrange("(a p j) r -> p a j r", p=P, j=PACK)
-        down_early = placed([P, 2, PACK, R], F32, "down_early", SLOT_E)
-        nc.sync.dma_start(out=down_early[:], in_=down_rows[:, 0:2, :, :])
-        down_last = placed([P, PACK, R], F32, "down_last", SLOT_W4 - 4)
-        nc.sync.dma_start(out=down_last[:], in_=down_rows[:, 2, :, :])
-        down_raw = [down_early[:, 0, :, :], down_early[:, 1, :, :], down_last[:]]
-
         tab_raw = []
 
-        def load_words(a, kib):
-            words = placed([P, T], I32, "tab_raw%d" % a, kib)
+        def load_words(a):
+            words = placed([P, T], I32, "tab_raw%d" % a, SLOT * a)
             nc.sync.dma_start(out=words[:], in_=tab_words[a].rearrange("p t i -> p (t i)").bitcast(I32))
             tab_raw.append(words)
 
-        load_words(0, SLOT_D)
+        load_words(0)
+        offsets = keep.tile([P, S // 16], U16, name="offsets")
+        nc.sync.dma_start(offsets[:], offs)
 
-        picked_scales = keep.tile([P, S], U8, name="picked_scales", align_bytes=64)
-        moved_scales = keep.tile([P, PASSES, S // 4], I32, name="moved_scales", align_bytes=64)
-        nc.vector.memset(moved_scales[:], 0)
-        nc.vector.tensor_copy(picked_scales[:], scale_window[:].bitcast(U8).indirect(offsets[:]))
+        scale_window = placed([P, PASSES, T // 4], I32, "scale_window", SPARE)
+        nc.vector.memset(scale_window[:], 0)
+        staged = placed([P, (V_BYTES + W4_BYTES) // 4], I32, "staged", SPARE + 18)
+        nc.scalar.dma_start(
+            out=staged[32:96:4, V_BYTES // 4 :].rearrange("q (a t) -> q a t", a=PASSES),
+            in_=w4_scales.bitcast(I32).rearrange("a q t -> q a t"),
+        )
+        nc.scalar.dma_start(
+            out=scale_window[32:96:4, :, :], in_=tab_scales.bitcast(I32).rearrange("a q t -> q a t")
+        )
+        down_raw = placed([P, PASSES, PACK, R], F32, "down_raw", SLOT * 3)
+        nc.sync.dma_start(out=down_raw[:], in_=down.rearrange("(a p j) r -> p a j r", p=P, j=PACK))
+        load_words(1)
+        load_words(2)
+        up_raw = placed([P, PACK, M], F32, "up_raw", SLOT * 7)
+        nc.sync.dma_start(out=up_raw[:], in_=up.rearrange("(p j) n -> p j n", j=PACK))
 
-        def move_scales(a, first_partition, step):
-            for r in range(4):
-                start = first_partition + step * r
-                nc.sync.dma_start(
-                    out=moved_scales[r:P:32, a, :],
-                    in_=picked_scales[start : start + 12 * step + 1 : 4 * step, :].bitcast(I32),
-                )
+        planes = keep.tile([P, (V_BYTES + W4_BYTES) // 4], I32, name="planes", align_bytes=64)
+        nc.vector.memset(planes[:], 0)
+        picked = placed([P, PASSES, S], U8, "picked", SPARE + 12)
+        for a in range(PASSES):
+            nc.vector.tensor_copy(picked[:, a, :], scale_window[:, a, :].bitcast(U8).indirect(offsets[:]))
+        nc.vector.tensor_copy(
+            out=staged[:, 0 : V_BYTES // 4], in_=picked[:].rearrange("p a s -> p (a s)").bitcast(I32)
+        )
+        for r in range(4):
+            nc.scalar.dma_start(out=planes[r:P:32, :], in_=staged[32 + 4 * r : 96 : 16, :])
+        plane_bytes = planes[:].bitcast(U8)
 
-        move_scales(0, 0, 4)
-        load_words(1, SLOT_A)
-        move_scales(1, 64, 4)
-        load_words(2, SLOT_B)
-        move_scales(2, 1, 8)
-        v_plane = [moved_scales[:, a, :].bitcast(U8) for a in range(PASSES)]
+        w4_codes = placed([P, PASSES, 2 * M], U8, "w4_codes", SPARE + 18)
+        nc.sync.dma_start(
+            out=w4_codes[:].bitcast(I32), in_=w4_words.bitcast(I32).rearrange("a p b -> p a b")
+        )
+
+        v_codes = keep.tile([P, PASSES, S], U32, name="v_codes", align_bytes=64)
+        nc.vector.tensor_copy(v_codes[:, 0, :], tab_raw[0][:].bitcast(U32).indirect(offsets[:]))
 
         down_codes = keep.tile([P, PASSES, R], U32, name="down_codes", align_bytes=64)
         down_plane = keep.tile([P, PASSES, R], U8, name="down_plane", align_bytes=64)
         for a in range(PASSES):
-            grouped = placed([P, R * PACK], BF16, "down_grouped%d" % a, STAGE + 4 * a)
+            grouped = placed([P, R * PACK], BF16, "down_grouped%d" % a, SLOT * 5 + 4 * a)
             nc.scalar.copy(
                 out=grouped[:].rearrange("p (t m j) -> p m j t", t=PACK, j=PACK),
-                in_=down_raw[a].rearrange("p j (m t) -> p m j t", t=PACK),
+                in_=down_raw[:, a, :, :].rearrange("p j (m t) -> p m j t", t=PACK),
             )
             nc.vector.quantize_mx(
                 out=down_codes[:, a, :].bitcast(FP8X4), scales=down_plane[:, a, :], in_=grouped[:]
             )
 
-        up_raw = placed([P, PACK, M], F32, "up_raw", SLOT_C)
-        nc.sync.dma_start(out=up_raw[:], in_=up.rearrange("(p j) n -> p j n", j=PACK))
-        w4_codes = placed([P, PASSES, 2 * M], U8, "w4_codes", SLOT_W4 + 3)
-        nc.sync.dma_start(
-            out=w4_codes[:].bitcast(I32), in_=w4_words.bitcast(I32).rearrange("a p b -> p a b")
-        )
-        w4_plane = placed([P, PASSES, M // 4], I32, "w4_plane", SLOT_W4)
-        nc.vector.memset(w4_plane[:], 0)
-        for r in range(4):
-            nc.sync.dma_start(
-                out=w4_plane[r:P:32, :, :],
-                in_=w4_scales.bitcast(I32)[:, r:16:4, :].rearrange("a q t -> q a t"),
-            )
-
-        v_codes = keep.tile([P, PASSES, S], U32, name="v_codes", align_bytes=64)
-        for a in range(PASSES - 1):
-            nc.vector.tensor_copy(v_codes[:, a, :], tab_raw[a][:].bitcast(U32).indirect(offsets[:]))
+        nc.vector.tensor_copy(v_codes[:, 1, :], tab_raw[1][:].bitcast(U32).indirect(offsets[:]))
         a = PASSES - 1
         for c in range(CHUNKS):
             nc.vector.tensor_copy(
@@ -129,7 +117,7 @@ def tile_list_tabgate_none_kernel(
         up_plane = keep.tile([P, M], U8, name="up_plane", align_bytes=64)
         for half in range(2):
             cols = slice(512 * half, 512 * (half + 1))
-            grouped = placed([P, 512 * PACK], BF16, "up_grouped%d" % half, (STAGE, SLOT_E)[half])
+            grouped = placed([P, 512 * PACK], BF16, "up_grouped%d" % half, SLOT * 6 + 4 * half)
             nc.vector.tensor_copy(
                 out=grouped[:].rearrange("p (c i j) -> p c j i", i=4, j=PACK),
                 in_=up_raw[:, :, cols].rearrange("p j (c i) -> p c j i", i=4),
@@ -140,9 +128,9 @@ def tile_list_tabgate_none_kernel(
         h_plane = keep.tile([P, S], U8, name="h_plane", align_bytes=64)
 
         def make_h(c):
-            grouped = placed([P, CHUNK * PACK], BF16, "h_grouped%d" % c, (STAGE + 4, STAGE + 8, SLOT_F)[c])
+            grouped = placed([P, CHUNK * PACK], BF16, "h_grouped%d" % c, SPARE + 4 * c)
             for b in range(CHUNK // H_COLS):
-                cols = slice(CHUNK * c + H_COLS * b, CHUNK * c + H_COLS * (b + 1))
+                first = CHUNK * c + H_COLS * b
                 bank = psum_h.tile([P, PACK, H_COLS], F32, name="h_bank")
                 for t in range(PACK):
                     for a in range(PASSES):
@@ -150,8 +138,8 @@ def tile_list_tabgate_none_kernel(
                             out=bank[:, t, :],
                             lhsT=down_codes[:, a, P * t : P * (t + 1)].bitcast(FP8X4),
                             lhsT_scale=down_plane[:, a, P * t : P * (t + 1)],
-                            rhs=v_codes[:, a, cols].bitcast(FP8X4),
-                            rhs_scale=v_plane[a][:, cols],
+                            rhs=v_codes[:, a, first : first + H_COLS].bitcast(FP8X4),
+                            rhs_scale=plane_bytes[:, S * a + first : S * a + first + H_COLS],
                             start=(a == 0),
                             stop=(a == PASSES - 1),
                         )
@@ -163,61 +151,48 @@ def tile_list_tabgate_none_kernel(
             nc.vector.quantize_mx(out=h_codes[:, cols].bitcast(FP8X4), scales=h_plane[:, cols], in_=grouped[:])
 
         gates = []
-
-        def load_gates(m):
-            gate_rows = placed([P, T], F32, "gates%d" % m, GATE_SLOTS[m])
-            (nc.scalar, nc.sync)[m % 2].dma_start(out=gate_rows[:], in_=gT[P * m : P * (m + 1), :])
+        for m in range(M_TILES):
+            gate_rows = placed([P, T], F32, "gates%d" % m, SLOT * m)
+            nc.sync.dma_start(out=gate_rows[:], in_=gT[P * m : P * (m + 1), :])
             gates.append(gate_rows)
 
-        result = keep.tile([P, M_TILES, S], F32, name="result")
-        y_tiles = []
+        for c in range(CHUNKS):
+            make_h(c)
 
-        def make_out(m, c):
-            rows = slice(P * m, P * (m + 1))
-            cols = slice(CHUNK * c, CHUNK * (c + 1))
-            if c == 0:
-                y_tiles.append(ring.tile([P, S], F32, name="y_sb", tag="y_sb"))
-            acc = psum_y.tile([P, CHUNK], F32, name="y_bank")
-            for a in range(PASSES):
+        def make_y(m):
+            y_sb = ring.tile([P, S], F32, name="y_sb")
+            for c in range(CHUNKS):
+                cols = slice(CHUNK * c, CHUNK * (c + 1))
+                acc = psum_y.tile([P, CHUNK], F32, name="y_bank")
+                for a in range(PASSES):
+                    w4_first = V_BYTES + M * a + P * m
+                    nc.tensor.matmul_mx(
+                        out=acc[:],
+                        lhsT=w4_codes[:, a, 2 * P * m : 2 * P * (m + 1)].bitcast(FP4X4),
+                        lhsT_scale=plane_bytes[:, w4_first : w4_first + P],
+                        rhs=v_codes[:, a, cols].bitcast(FP8X4),
+                        rhs_scale=plane_bytes[:, S * a + CHUNK * c : S * a + CHUNK * (c + 1)],
+                        start=(a == 0),
+                        stop=False,
+                    )
                 nc.tensor.matmul_mx(
                     out=acc[:],
-                    lhsT=w4_codes[:, a, 2 * P * m : 2 * P * (m + 1)].bitcast(FP4X4),
-                    lhsT_scale=w4_plane[:, a, :].bitcast(U8)[:, rows],
-                    rhs=v_codes[:, a, cols].bitcast(FP8X4),
-                    rhs_scale=v_plane[a][:, cols],
-                    start=(a == 0),
-                    stop=False,
+                    lhsT=up_codes[:, P * m : P * (m + 1)].bitcast(FP8X4),
+                    lhsT_scale=up_plane[:, P * m : P * (m + 1)],
+                    rhs=h_codes[:, cols].bitcast(FP8X4),
+                    rhs_scale=h_plane[:, cols],
+                    start=False,
+                    stop=True,
                 )
-            nc.tensor.matmul_mx(
-                out=acc[:],
-                lhsT=up_codes[:, rows].bitcast(FP8X4),
-                lhsT_scale=up_plane[:, rows],
-                rhs=h_codes[:, cols].bitcast(FP8X4),
-                rhs_scale=h_plane[:, cols],
-                start=False,
-                stop=True,
-            )
-            nc.scalar.copy(out=y_tiles[m][:, cols], in_=acc[:])
-            nc.vector.tensor_tensor(
-                result[:, m, cols],
-                gates[m][:].indirect(offsets[:, LIST_COLS * c : LIST_COLS * (c + 1)]),
-                y_tiles[m][:, cols],
-                MULT,
-            )
+                nc.scalar.copy(out=y_sb[:, cols], in_=acc[:])
+            return y_sb
 
         out_rows = out.rearrange("(m p) s -> p m s", p=P)
-        for m in range(5):
-            load_gates(m)
-        make_h(0)
-        make_h(1)
-        make_out(0, 0)
-        make_out(0, 1)
-        make_h(2)
-        for m in range(5, M_TILES):
-            load_gates(m)
-        make_out(0, 2)
-        for m in range(1, M_TILES):
-            for c in range(CHUNKS):
-                make_out(m, c)
-            if m in STORE_FROM:
-                (nc.scalar, nc.sync)[m % 2].dma_start(out=out_rows[:, STORE_FROM[m] : m + 1, :], in_=result[:, STORE_FROM[m] : m + 1, :])
+        for first, last, kib in STORE_GROUPS:
+            result = placed([P, last - first, S], F32, "result%d" % first, kib)
+            for m in range(first, last):
+                y_sb = make_y(m)
+                nc.vector.tensor_tensor(
+                    result[:, m - first, :], gates[m][:].indirect(offsets[:]), y_sb[:], MULT
+                )
+            nc.sync.dma_start(out=out_rows[:, first:last, :], in_=result[:])

@@ -26,9 +26,8 @@ LIST_COLS = CHUNK // 16
 
 SLOT = 16
 SPARE = SLOT * M_TILES
-V_BYTES = PASSES * S
-W4_BYTES = PASSES * M
-STORE_GROUPS = ((0, 3, SPARE), (3, 6, 0), (6, 7, 18), (7, 8, 24))
+GATE_SLOTS = (7, 2, 3, 4, 0, 1, 5, 6)
+STORE_GROUPS = ((0, 3, SPARE + 11), (3, 6, 32), (6, 7, 50), (7, 8, 56))
 
 
 def tile_list_tabgate_none_kernel(
@@ -43,60 +42,67 @@ def tile_list_tabgate_none_kernel(
         psum_y = ctx.enter_context(tc.psum_pool(name="psum_y", bufs=5))
 
         def placed(shape, dtype, name, kib):
-            return arena.tile(shape, dtype, name=name, offset=1024 * kib, align_bytes=64)
+            return arena.tile(shape, dtype, name=name, offset=int(1024 * kib), align_bytes=64)
 
-        tab_raw = []
-
-        def load_words(a):
-            words = placed([P, T], I32, "tab_raw%d" % a, SLOT * a)
-            nc.sync.dma_start(out=words[:], in_=tab_words[a].rearrange("p t i -> p (t i)").bitcast(I32))
-            tab_raw.append(words)
-
-        load_words(0)
+        scale_rows = tab_scales.bitcast(I32).rearrange("a q t -> (a q) t")
+        scale_window = placed([P, T // 4], I32, "scale_window", SPARE - 0.5)
+        nc.sync.dma_start(out=scale_window[64:96, :], in_=scale_rows[0:32, :])
+        nc.sync.dma_start(out=scale_window[16:32, :], in_=scale_rows[32:48, :])
+        for first, last in ((0, 16), (32, 64), (96, 128)):
+            nc.vector.memset(scale_window[first:last, :], 0)
         offsets = keep.tile([P, S // 16], U16, name="offsets")
         nc.sync.dma_start(offsets[:], offs)
 
-        scale_window = placed([P, PASSES, T // 4], I32, "scale_window", SPARE)
-        nc.vector.memset(scale_window[:], 0)
-        staged = placed([P, (V_BYTES + W4_BYTES) // 4], I32, "staged", SPARE + 18)
-        nc.scalar.dma_start(
-            out=staged[32:96:4, V_BYTES // 4 :].rearrange("q (a t) -> q a t", a=PASSES),
-            in_=w4_scales.bitcast(I32).rearrange("a q t -> q a t"),
-        )
-        nc.scalar.dma_start(
-            out=scale_window[32:96:4, :, :], in_=tab_scales.bitcast(I32).rearrange("a q t -> q a t")
-        )
-        down_raw = placed([P, PASSES, PACK, R], F32, "down_raw", SLOT * 3)
+        tab_raw = []
+
+        def load_words(a, kib):
+            words = placed([P, T], I32, "tab_raw%d" % a, kib)
+            nc.sync.dma_start(out=words[:], in_=tab_words[a].rearrange("p t i -> p (t i)").bitcast(I32))
+            tab_raw.append(words)
+
+        load_words(0, SLOT - 1)
+        down_raw = placed([P, PASSES, PACK, R], F32, "down_raw", SLOT * 2)
         nc.sync.dma_start(out=down_raw[:], in_=down.rearrange("(a p j) r -> p a j r", p=P, j=PACK))
-        load_words(1)
-        load_words(2)
-        up_raw = placed([P, PACK, M], F32, "up_raw", SLOT * 7)
-        nc.sync.dma_start(out=up_raw[:], in_=up.rearrange("(p j) n -> p j n", j=PACK))
 
-        planes = keep.tile([P, (V_BYTES + W4_BYTES) // 4], I32, name="planes", align_bytes=64)
-        nc.vector.memset(planes[:], 0)
-        picked = placed([P, PASSES, S], U8, "picked", SPARE + 12)
-        for a in range(PASSES):
-            nc.vector.tensor_copy(picked[:, a, :], scale_window[:, a, :].bitcast(U8).indirect(offsets[:]))
-        nc.vector.tensor_copy(
-            out=staged[:, 0 : V_BYTES // 4], in_=picked[:].rearrange("p a s -> p (a s)").bitcast(I32)
-        )
-        for r in range(4):
-            nc.scalar.dma_start(out=planes[r:P:32, :], in_=staged[32 + 4 * r : 96 : 16, :])
-        plane_bytes = planes[:].bitcast(U8)
+        v_planes = keep.tile([P, PASSES, S // 4], I32, name="v_planes", align_bytes=64)
+        nc.vector.memset(v_planes[:], 0)
+        picked = placed([P, S], U8, "picked", SPARE + 9)
+        nc.vector.tensor_copy(picked[:], scale_window[:].bitcast(U8).indirect(offsets[:]))
 
-        w4_codes = placed([P, PASSES, 2 * M], U8, "w4_codes", SPARE + 18)
-        nc.sync.dma_start(
-            out=w4_codes[:].bitcast(I32), in_=w4_words.bitcast(I32).rearrange("a p b -> p a b")
-        )
+        def move_scales(a, first):
+            for r in range(4):
+                nc.sync.dma_start(
+                    out=v_planes[r:P:32, a, :], in_=picked[first + r : first + 16 : 4, :].bitcast(I32)
+                )
 
         v_codes = keep.tile([P, PASSES, S], U32, name="v_codes", align_bytes=64)
         nc.vector.tensor_copy(v_codes[:, 0, :], tab_raw[0][:].bitcast(U32).indirect(offsets[:]))
 
+        move_scales(0, 64)
+        load_words(1, SLOT * 7)
+        move_scales(1, 80)
+        load_words(2, 0)
+        move_scales(2, 16)
+        up_raw = placed([P, PACK, M], F32, "up_raw", SLOT)
+        nc.sync.dma_start(out=up_raw[:], in_=up.rearrange("(p j) n -> p j n", j=PACK))
+        w4_codes = placed([P, PASSES, 2 * M], U8, "w4_codes", SPARE + 3)
+        nc.sync.dma_start(
+            out=w4_codes[:].bitcast(I32), in_=w4_words.bitcast(I32).rearrange("a p b -> p a b")
+        )
+        w4_planes = placed([P, PASSES, M // 4], I32, "w4_planes", SPARE)
+        nc.vector.memset(w4_planes[:], 0)
+        for r in range(4):
+            nc.sync.dma_start(
+                out=w4_planes[r:P:32, :, :],
+                in_=w4_scales.bitcast(I32)[:, r:16:4, :].rearrange("a q t -> q a t"),
+            )
+        v_plane = [v_planes[:, a, :].bitcast(U8) for a in range(PASSES)]
+        w4_plane = [w4_planes[:, a, :].bitcast(U8) for a in range(PASSES)]
+
         down_codes = keep.tile([P, PASSES, R], U32, name="down_codes", align_bytes=64)
         down_plane = keep.tile([P, PASSES, R], U8, name="down_plane", align_bytes=64)
         for a in range(PASSES):
-            grouped = placed([P, R * PACK], BF16, "down_grouped%d" % a, SLOT * 5 + 4 * a)
+            grouped = placed([P, R * PACK], BF16, "down_grouped%d" % a, SLOT * 4 + 4 * a)
             nc.scalar.copy(
                 out=grouped[:].rearrange("p (t m j) -> p m j t", t=PACK, j=PACK),
                 in_=down_raw[:, a, :, :].rearrange("p j (m t) -> p m j t", t=PACK),
@@ -117,7 +123,7 @@ def tile_list_tabgate_none_kernel(
         up_plane = keep.tile([P, M], U8, name="up_plane", align_bytes=64)
         for half in range(2):
             cols = slice(512 * half, 512 * (half + 1))
-            grouped = placed([P, 512 * PACK], BF16, "up_grouped%d" % half, SLOT * 6 + 4 * half)
+            grouped = placed([P, 512 * PACK], BF16, "up_grouped%d" % half, SLOT * 5 + 4 * half)
             nc.vector.tensor_copy(
                 out=grouped[:].rearrange("p (c i j) -> p c j i", i=4, j=PACK),
                 in_=up_raw[:, :, cols].rearrange("p j (c i) -> p c j i", i=4),
@@ -128,7 +134,7 @@ def tile_list_tabgate_none_kernel(
         h_plane = keep.tile([P, S], U8, name="h_plane", align_bytes=64)
 
         def make_h(c):
-            grouped = placed([P, CHUNK * PACK], BF16, "h_grouped%d" % c, SPARE + 4 * c)
+            grouped = placed([P, CHUNK * PACK], BF16, "h_grouped%d" % c, SLOT * 6 + 4 * c)
             for b in range(CHUNK // H_COLS):
                 first = CHUNK * c + H_COLS * b
                 bank = psum_h.tile([P, PACK, H_COLS], F32, name="h_bank")
@@ -139,7 +145,7 @@ def tile_list_tabgate_none_kernel(
                             lhsT=down_codes[:, a, P * t : P * (t + 1)].bitcast(FP8X4),
                             lhsT_scale=down_plane[:, a, P * t : P * (t + 1)],
                             rhs=v_codes[:, a, first : first + H_COLS].bitcast(FP8X4),
-                            rhs_scale=plane_bytes[:, S * a + first : S * a + first + H_COLS],
+                            rhs_scale=v_plane[a][:, first : first + H_COLS],
                             start=(a == 0),
                             stop=(a == PASSES - 1),
                         )
@@ -150,14 +156,14 @@ def tile_list_tabgate_none_kernel(
             cols = slice(CHUNK * c, CHUNK * (c + 1))
             nc.vector.quantize_mx(out=h_codes[:, cols].bitcast(FP8X4), scales=h_plane[:, cols], in_=grouped[:])
 
-        gates = []
-        for m in range(M_TILES):
-            gate_rows = placed([P, T], F32, "gates%d" % m, SLOT * m)
-            nc.sync.dma_start(out=gate_rows[:], in_=gT[P * m : P * (m + 1), :])
-            gates.append(gate_rows)
-
         for c in range(CHUNKS):
             make_h(c)
+
+        gates = []
+        for m in range(M_TILES):
+            gate_rows = placed([P, T], F32, "gates%d" % m, SLOT * GATE_SLOTS[m])
+            nc.sync.dma_start(out=gate_rows[:], in_=gT[P * m : P * (m + 1), :])
+            gates.append(gate_rows)
 
         def make_y(m):
             y_sb = ring.tile([P, S], F32, name="y_sb")
@@ -165,13 +171,12 @@ def tile_list_tabgate_none_kernel(
                 cols = slice(CHUNK * c, CHUNK * (c + 1))
                 acc = psum_y.tile([P, CHUNK], F32, name="y_bank")
                 for a in range(PASSES):
-                    w4_first = V_BYTES + M * a + P * m
                     nc.tensor.matmul_mx(
                         out=acc[:],
                         lhsT=w4_codes[:, a, 2 * P * m : 2 * P * (m + 1)].bitcast(FP4X4),
-                        lhsT_scale=plane_bytes[:, w4_first : w4_first + P],
+                        lhsT_scale=w4_plane[a][:, P * m : P * (m + 1)],
                         rhs=v_codes[:, a, cols].bitcast(FP8X4),
-                        rhs_scale=plane_bytes[:, S * a + CHUNK * c : S * a + CHUNK * (c + 1)],
+                        rhs_scale=v_plane[a][:, cols],
                         start=(a == 0),
                         stop=False,
                     )

@@ -24,6 +24,8 @@ H_COLS = 128
 M_TILES = M // P
 LIST_COLS = CHUNK // 16
 
+BANK = 2048
+BANKS = 8
 SLOT = 16
 SPARE = SLOT * M_TILES
 GATE_SLOTS = (7, 2, 3, 4, 0, 1, 5, 6)
@@ -38,8 +40,7 @@ def tile_list_tabgate_none_kernel(
         keep = ctx.enter_context(tc.tile_pool(name="keep", bufs=1))
         arena = ctx.enter_context(tc.tile_pool(name="arena", bufs=1))
         ring = ctx.enter_context(tc.tile_pool(name="ring", bufs=4))
-        psum_h = ctx.enter_context(tc.psum_pool(name="psum_h", bufs=3))
-        psum_y = ctx.enter_context(tc.psum_pool(name="psum_y", bufs=5))
+        psum = ctx.enter_context(tc.psum_pool(name="psum", bufs=1))
 
         def placed(shape, dtype, name, kib):
             return arena.tile(shape, dtype, name=name, offset=int(1024 * kib), align_bytes=64)
@@ -133,11 +134,11 @@ def tile_list_tabgate_none_kernel(
         h_codes = keep.tile([P, S], U32, name="h_codes", align_bytes=64)
         h_plane = keep.tile([P, S], U8, name="h_plane", align_bytes=64)
 
-        def make_h(c):
+        def make_h(c, banks):
             grouped = placed([P, CHUNK * PACK], BF16, "h_grouped%d" % c, SLOT * 6 + 4 * c)
             for b in range(CHUNK // H_COLS):
                 first = CHUNK * c + H_COLS * b
-                bank = psum_h.tile([P, PACK, H_COLS], F32, name="h_bank")
+                bank = psum.tile([P, PACK, H_COLS], F32, name="h_bank", offset=BANK * banks[b])
                 for t in range(PACK):
                     for a in range(PASSES):
                         nc.tensor.matmul_mx(
@@ -156,48 +157,71 @@ def tile_list_tabgate_none_kernel(
             cols = slice(CHUNK * c, CHUNK * (c + 1))
             nc.vector.quantize_mx(out=h_codes[:, cols].bitcast(FP8X4), scales=h_plane[:, cols], in_=grouped[:])
 
-        for c in range(CHUNKS):
-            make_h(c)
+        def make_y(m, c, y_sb, bank):
+            cols = slice(CHUNK * c, CHUNK * (c + 1))
+            acc = psum.tile([P, CHUNK], F32, name="y_bank", offset=BANK * bank)
+            for a in range(PASSES):
+                nc.tensor.matmul_mx(
+                    out=acc[:],
+                    lhsT=w4_codes[:, a, 2 * P * m : 2 * P * (m + 1)].bitcast(FP4X4),
+                    lhsT_scale=w4_plane[a][:, P * m : P * (m + 1)],
+                    rhs=v_codes[:, a, cols].bitcast(FP8X4),
+                    rhs_scale=v_plane[a][:, cols],
+                    start=(a == 0),
+                    stop=False,
+                )
+            nc.tensor.matmul_mx(
+                out=acc[:],
+                lhsT=up_codes[:, P * m : P * (m + 1)].bitcast(FP8X4),
+                lhsT_scale=up_plane[:, P * m : P * (m + 1)],
+                rhs=h_codes[:, cols].bitcast(FP8X4),
+                rhs_scale=h_plane[:, cols],
+                start=False,
+                stop=True,
+            )
+            nc.scalar.copy(out=y_sb[:, cols], in_=acc[:])
 
         gates = []
-        for m in range(M_TILES):
+
+        def load_gates(m):
             gate_rows = placed([P, T], F32, "gates%d" % m, SLOT * GATE_SLOTS[m])
             nc.sync.dma_start(out=gate_rows[:], in_=gT[P * m : P * (m + 1), :])
             gates.append(gate_rows)
 
-        def make_y(m):
-            y_sb = ring.tile([P, S], F32, name="y_sb")
-            for c in range(CHUNKS):
-                cols = slice(CHUNK * c, CHUNK * (c + 1))
-                acc = psum_y.tile([P, CHUNK], F32, name="y_bank")
-                for a in range(PASSES):
-                    nc.tensor.matmul_mx(
-                        out=acc[:],
-                        lhsT=w4_codes[:, a, 2 * P * m : 2 * P * (m + 1)].bitcast(FP4X4),
-                        lhsT_scale=w4_plane[a][:, P * m : P * (m + 1)],
-                        rhs=v_codes[:, a, cols].bitcast(FP8X4),
-                        rhs_scale=v_plane[a][:, cols],
-                        start=(a == 0),
-                        stop=False,
-                    )
-                nc.tensor.matmul_mx(
-                    out=acc[:],
-                    lhsT=up_codes[:, P * m : P * (m + 1)].bitcast(FP8X4),
-                    lhsT_scale=up_plane[:, P * m : P * (m + 1)],
-                    rhs=h_codes[:, cols].bitcast(FP8X4),
-                    rhs_scale=h_plane[:, cols],
-                    start=False,
-                    stop=True,
-                )
-                nc.scalar.copy(out=y_sb[:, cols], in_=acc[:])
-            return y_sb
+        def gate(result, m, y_sb, first, last):
+            cols = slice(CHUNK * first, CHUNK * last)
+            nc.vector.tensor_tensor(
+                result[:, cols],
+                gates[m][:].indirect(offsets[:, LIST_COLS * first : LIST_COLS * last]),
+                y_sb[:, cols],
+                MULT,
+            )
 
+        make_h(0, (0, 1, 2, 3))
+        make_h(1, (4, 5, 6, 7))
+        for m in range(M_TILES - 1):
+            load_gates(m)
         out_rows = out.rearrange("(m p) s -> p m s", p=P)
+        first, last, kib = STORE_GROUPS[0]
+        result = placed([P, last - first, S], F32, "result0", kib)
+        early = [ring.tile([P, S], F32, name="y_sb") for m in range(2)]
+        for c in range(2):
+            make_y(0, c, early[0], c)
+            gate(result[:, 0, :], 0, early[0], c, c + 1)
+        make_h(2, (0, 1, 0, 1))
+        load_gates(M_TILES - 1)
+        for c in range(2):
+            make_y(1, c, early[1], 2 + c)
+            gate(result[:, 1, :], 1, early[1], c, c + 1)
+        for m in range(2):
+            make_y(m, 2, early[m], 4 + m)
+            gate(result[:, m, :], m, early[m], 2, 3)
         for first, last, kib in STORE_GROUPS:
-            result = placed([P, last - first, S], F32, "result%d" % first, kib)
-            for m in range(first, last):
-                y_sb = make_y(m)
-                nc.vector.tensor_tensor(
-                    result[:, m - first, :], gates[m][:].indirect(offsets[:]), y_sb[:], MULT
-                )
+            if first > 0:
+                result = placed([P, last - first, S], F32, "result%d" % first, kib)
+            for m in range(max(first, 2), last):
+                y_sb = ring.tile([P, S], F32, name="y_sb")
+                for c in range(CHUNKS):
+                    make_y(m, c, y_sb, (CHUNKS * m + c) % BANKS)
+                gate(result[:, m - first, :], m, y_sb, 0, CHUNKS)
             nc.sync.dma_start(out=out_rows[:, first:last, :], in_=result[:])

@@ -27,9 +27,14 @@ LIST_COLS = CHUNK // 16
 BANK = 2048
 BANKS = 8
 SLOT = 16
-SPARE = SLOT * M_TILES
-GATE_SLOTS = (7, 2, 3, 4, 0, 1, 5, 6)
-STORE_GROUPS = ((0, 3, SPARE + 11), (3, 6, 32), (6, 7, 50), (7, 8, 56))
+SLOTS = 20
+W4_AT = SLOTS + SLOT * (M_TILES - 1)
+SPARE = W4_AT + 6 + SLOT
+V_WORDS = PASSES * S // 4
+W4_WORDS = PASSES * M // 4
+GATE_AT = tuple(SLOTS + SLOT * i for i in (6, 7, 1, 2, 3, 0, 4, 5))
+GATE_AT = GATE_AT[:1] + (W4_AT + 6,) + GATE_AT[2:]
+STORE_GROUPS = ((0, 4, SPARE), (4, 7, SLOTS + SLOT), (7, 8, SLOTS + SLOT * 6))
 
 
 def tile_list_tabgate_none_kernel(
@@ -45,87 +50,77 @@ def tile_list_tabgate_none_kernel(
         def placed(shape, dtype, name, kib):
             return arena.tile(shape, dtype, name=name, offset=int(1024 * kib), align_bytes=64)
 
-        scale_rows = tab_scales.bitcast(I32).rearrange("a q t -> (a q) t")
-        scale_window = placed([P, T // 4], I32, "scale_window", SPARE - 0.5)
-        nc.sync.dma_start(out=scale_window[64:96, :], in_=scale_rows[0:32, :])
-        nc.sync.dma_start(out=scale_window[16:32, :], in_=scale_rows[32:48, :])
-        for first, last in ((0, 16), (32, 64), (96, 128)):
-            nc.vector.memset(scale_window[first:last, :], 0)
+        down_rows = down.rearrange("(a p j) r -> p a j r", p=P, j=PACK)
+        down_first = placed([P, PACK, R], F32, "down_first", SLOTS + SLOT)
+        nc.sync.dma_start(out=down_first[:], in_=down_rows[:, 0, :, :])
         offsets = keep.tile([P, S // 16], U16, name="offsets")
         nc.sync.dma_start(offsets[:], offs)
+        down_rest = placed([P, PASSES - 1, PACK, R], F32, "down_rest", SPARE + 12)
+        nc.sync.dma_start(out=down_rest[:], in_=down_rows[:, 1:PASSES, :, :])
+        down_raw = [down_first[:], down_rest[:, 0, :, :], down_rest[:, 1, :, :]]
 
-        tab_raw = []
+        staged = placed([P, V_WORDS + W4_WORDS], I32, "staged", W4_AT - 0.75)
+        nc.sync.dma_start(
+            out=staged[32:96:4, V_WORDS:].rearrange("q (a t) -> q a t", a=PASSES),
+            in_=w4_scales.bitcast(I32).rearrange("a q t -> q a t"),
+        )
+        scale_window = placed([P, PASSES, T // 4], I32, "scale_window", SPARE)
+        nc.vector.memset(scale_window[:], 0)
+        nc.sync.dma_start(
+            out=scale_window[32:96:4, :, :], in_=tab_scales.bitcast(I32).rearrange("a q t -> q a t")
+        )
+        planes = keep.tile([P, V_WORDS + W4_WORDS], I32, name="planes", align_bytes=64)
+        nc.vector.memset(planes[:], 0)
 
-        def load_words(a, kib):
-            words = placed([P, T], I32, "tab_raw%d" % a, kib)
-            nc.sync.dma_start(out=words[:], in_=tab_words[a].rearrange("p t i -> p (t i)").bitcast(I32))
-            tab_raw.append(words)
+        down_grouped = []
+        for a in range(PASSES):
+            grouped = placed([P, R * PACK], BF16, "down_grouped%d" % a, SLOTS + SLOT * 5 + 4 * a)
+            nc.scalar.copy(
+                out=grouped[:].rearrange("p (t m j) -> p m j t", t=PACK, j=PACK),
+                in_=down_raw[a].rearrange("p j (m t) -> p m j t", t=PACK),
+            )
+            down_grouped.append(grouped)
 
-        load_words(0, SLOT - 1)
-        down_raw = placed([P, PASSES, PACK, R], F32, "down_raw", SLOT * 2)
-        nc.sync.dma_start(out=down_raw[:], in_=down.rearrange("(a p j) r -> p a j r", p=P, j=PACK))
+        words = placed([P, PASSES, T], I32, "words", SLOTS + SLOT)
+        nc.sync.dma_start(out=words[:], in_=tab_words.rearrange("a p t i -> p a (t i)").bitcast(I32))
 
-        v_planes = keep.tile([P, PASSES, S // 4], I32, name="v_planes", align_bytes=64)
-        nc.vector.memset(v_planes[:], 0)
-        picked = placed([P, S], U8, "picked", SPARE + 9)
-        nc.vector.tensor_copy(picked[:], scale_window[:].bitcast(U8).indirect(offsets[:]))
-
-        def move_scales(a, first):
-            for r in range(4):
-                nc.sync.dma_start(
-                    out=v_planes[r:P:32, a, :], in_=picked[first + r : first + 16 : 4, :].bitcast(I32)
-                )
-
-        v_codes = keep.tile([P, PASSES, S], U32, name="v_codes", align_bytes=64)
-        nc.vector.tensor_copy(v_codes[:, 0, :], tab_raw[0][:].bitcast(U32).indirect(offsets[:]))
-
-        move_scales(0, 64)
-        load_words(1, SLOT * 7)
-        move_scales(1, 80)
-        load_words(2, 0)
-        move_scales(2, 16)
-        up_raw = placed([P, PACK, M], F32, "up_raw", SLOT)
+        picked = placed([P, PASSES, S], U8, "picked", 17.5)
+        for a in range(PASSES):
+            nc.vector.tensor_copy(picked[:, a, :], scale_window[:, a, :].bitcast(U8).indirect(offsets[:]))
+        nc.vector.tensor_copy(out=staged[:, 0:V_WORDS], in_=picked[:].rearrange("p a s -> p (a s)").bitcast(I32))
+        for r in range(4):
+            nc.sync.dma_start(out=planes[r:P:32, :], in_=staged[32 + 4 * r : 96 : 16, :])
+        up_raw = placed([P, PACK, M], F32, "up_raw", SLOTS)
         nc.sync.dma_start(out=up_raw[:], in_=up.rearrange("(p j) n -> p j n", j=PACK))
-        w4_codes = placed([P, PASSES, 2 * M], U8, "w4_codes", SPARE + 3)
+        w4_codes = placed([P, PASSES, 2 * M], U8, "w4_codes", W4_AT)
         nc.sync.dma_start(
             out=w4_codes[:].bitcast(I32), in_=w4_words.bitcast(I32).rearrange("a p b -> p a b")
         )
-        w4_planes = placed([P, PASSES, M // 4], I32, "w4_planes", SPARE)
-        nc.vector.memset(w4_planes[:], 0)
-        for r in range(4):
-            nc.sync.dma_start(
-                out=w4_planes[r:P:32, :, :],
-                in_=w4_scales.bitcast(I32)[:, r:16:4, :].rearrange("a q t -> q a t"),
-            )
-        v_plane = [v_planes[:, a, :].bitcast(U8) for a in range(PASSES)]
-        w4_plane = [w4_planes[:, a, :].bitcast(U8) for a in range(PASSES)]
+        plane_bytes = planes[:].bitcast(U8)
+        v_plane = [plane_bytes[:, S * a : S * (a + 1)] for a in range(PASSES)]
+        w4_plane = [plane_bytes[:, PASSES * S + M * a : PASSES * S + M * (a + 1)] for a in range(PASSES)]
 
         down_codes = keep.tile([P, PASSES, R], U32, name="down_codes", align_bytes=64)
-        down_plane = keep.tile([P, PASSES, R], U8, name="down_plane", align_bytes=64)
+        down_plane = placed([P, PASSES, R], U8, "down_plane", 18)
         for a in range(PASSES):
-            grouped = placed([P, R * PACK], BF16, "down_grouped%d" % a, SLOT * 4 + 4 * a)
-            nc.scalar.copy(
-                out=grouped[:].rearrange("p (t m j) -> p m j t", t=PACK, j=PACK),
-                in_=down_raw[:, a, :, :].rearrange("p j (m t) -> p m j t", t=PACK),
-            )
             nc.vector.quantize_mx(
-                out=down_codes[:, a, :].bitcast(FP8X4), scales=down_plane[:, a, :], in_=grouped[:]
+                out=down_codes[:, a, :].bitcast(FP8X4), scales=down_plane[:, a, :], in_=down_grouped[a][:]
             )
 
-        nc.vector.tensor_copy(v_codes[:, 1, :], tab_raw[1][:].bitcast(U32).indirect(offsets[:]))
-        a = PASSES - 1
+        v_codes = placed([P, PASSES, S], U32, "v_codes", 0)
         for c in range(CHUNKS):
-            nc.vector.tensor_copy(
-                v_codes[:, a, CHUNK * c : CHUNK * (c + 1)],
-                tab_raw[a][:].bitcast(U32).indirect(offsets[:, LIST_COLS * c : LIST_COLS * (c + 1)]),
-            )
+            for a in range(PASSES):
+                nc.vector.tensor_copy(
+                    v_codes[:, a, CHUNK * c : CHUNK * (c + 1)],
+                    words[:, a, :].bitcast(U32).indirect(offsets[:, LIST_COLS * c : LIST_COLS * (c + 1)]),
+                )
 
         up_codes = keep.tile([P, M], U32, name="up_codes", align_bytes=64)
         up_plane = keep.tile([P, M], U8, name="up_plane", align_bytes=64)
         for half in range(2):
             cols = slice(512 * half, 512 * (half + 1))
-            grouped = placed([P, 512 * PACK], BF16, "up_grouped%d" % half, SLOT * 5 + 4 * half)
-            nc.vector.tensor_copy(
+            grouped = placed([P, 512 * PACK], BF16, "up_grouped%d" % half, SLOTS + SLOT * 4 + 4 * half)
+            nc.scalar.copy(
                 out=grouped[:].rearrange("p (c i j) -> p c j i", i=4, j=PACK),
                 in_=up_raw[:, :, cols].rearrange("p j (c i) -> p c j i", i=4),
             )
@@ -135,7 +130,7 @@ def tile_list_tabgate_none_kernel(
         h_plane = keep.tile([P, S], U8, name="h_plane", align_bytes=64)
 
         def make_h(c, banks):
-            grouped = placed([P, CHUNK * PACK], BF16, "h_grouped%d" % c, SLOT * 6 + 4 * c)
+            grouped = placed([P, CHUNK * PACK], BF16, "h_grouped%d" % c, SLOTS + SLOT * 5 + 4 * c)
             for b in range(CHUNK // H_COLS):
                 first = CHUNK * c + H_COLS * b
                 bank = psum.tile([P, PACK, H_COLS], F32, name="h_bank", offset=BANK * banks[b])
@@ -184,7 +179,7 @@ def tile_list_tabgate_none_kernel(
         gates = []
 
         def load_gates(m):
-            gate_rows = placed([P, T], F32, "gates%d" % m, SLOT * GATE_SLOTS[m])
+            gate_rows = placed([P, T], F32, "gates%d" % m, GATE_AT[m])
             nc.sync.dma_start(out=gate_rows[:], in_=gT[P * m : P * (m + 1), :])
             gates.append(gate_rows)
 

@@ -74,7 +74,7 @@ def tile_list_tabgate_none_kernel(
 
         down_grouped = []
         for a in range(PASSES):
-            grouped = placed([P, R * PACK], BF16, "down_grouped%d" % a, SLOTS + SLOT * 5 + 4 * a)
+            grouped = placed([P, R * PACK], BF16, "down_grouped%d" % a, SLOTS + 4 if a == PASSES - 1 else SLOTS + SLOT * 5 + 4 * a)
             nc.scalar.copy(
                 out=grouped[:].rearrange("p (t m j) -> p m j t", t=PACK, j=PACK),
                 in_=down_raw[a].rearrange("p j (m t) -> p m j t", t=PACK),
@@ -90,12 +90,6 @@ def tile_list_tabgate_none_kernel(
         nc.vector.tensor_copy(out=staged[:, 0:V_WORDS], in_=picked[:].rearrange("p a s -> p (a s)").bitcast(I32))
         for r in range(4):
             nc.sync.dma_start(out=planes[r:P:32, :], in_=staged[32 + 4 * r : 96 : 16, :])
-        up_raw = placed([P, PACK, M], F32, "up_raw", SLOTS)
-        nc.sync.dma_start(out=up_raw[:], in_=up.rearrange("(p j) n -> p j n", j=PACK))
-        w4_codes = placed([P, PASSES, 2 * M], U8, "w4_codes", W4_AT)
-        nc.sync.dma_start(
-            out=w4_codes[:].bitcast(I32), in_=w4_words.bitcast(I32).rearrange("a p b -> p a b")
-        )
         plane_bytes = planes[:].bitcast(U8)
         v_plane = [plane_bytes[:, S * a : S * (a + 1)] for a in range(PASSES)]
         w4_plane = [plane_bytes[:, PASSES * S + M * a : PASSES * S + M * (a + 1)] for a in range(PASSES)]
@@ -106,6 +100,12 @@ def tile_list_tabgate_none_kernel(
             nc.vector.quantize_mx(
                 out=down_codes[:, a, :].bitcast(FP8X4), scales=down_plane[:, a, :], in_=down_grouped[a][:]
             )
+        up_raw = placed([P, PACK, M], F32, "up_raw", SLOTS)
+        nc.sync.dma_start(out=up_raw[:], in_=up.rearrange("(p j) n -> p j n", j=PACK))
+        w4_codes = placed([P, PASSES, 2 * M], U8, "w4_codes", W4_AT)
+        nc.sync.dma_start(
+            out=w4_codes[:].bitcast(I32), in_=w4_words.bitcast(I32).rearrange("a p b -> p a b")
+        )
 
         v_codes = placed([P, PASSES, S], U32, "v_codes", 0)
         for c in range(CHUNKS):

@@ -74,7 +74,7 @@ def tile_list_tabgate_none_kernel(
 
         down_grouped = []
         for a in range(PASSES):
-            grouped = placed([P, R * PACK], BF16, "down_grouped%d" % a, SLOTS + 4 if a == PASSES - 1 else SLOTS + SLOT * 5 + 4 * a)
+            grouped = placed([P, R * PACK], BF16, "down_grouped%d" % a, SLOTS + 4 if a == 0 else SLOTS + SLOT * 5 + 4 * a)
             nc.scalar.copy(
                 out=grouped[:].rearrange("p (t m j) -> p m j t", t=PACK, j=PACK),
                 in_=down_raw[a].rearrange("p j (m t) -> p m j t", t=PACK),
@@ -87,7 +87,7 @@ def tile_list_tabgate_none_kernel(
         picked = placed([P, PASSES, S], U8, "picked", 17.5)
         for a in range(PASSES):
             nc.vector.tensor_copy(picked[:, a, :], scale_window[:, a, :].bitcast(U8).indirect(offsets[:]))
-        nc.vector.tensor_copy(out=staged[:, 0:V_WORDS], in_=picked[:].rearrange("p a s -> p (a s)").bitcast(I32))
+            nc.vector.tensor_copy(out=staged[:, S // 4 * a : S // 4 * (a + 1)], in_=picked[:, a, :].bitcast(I32))
         for r in range(4):
             nc.sync.dma_start(out=planes[r:P:32, :], in_=staged[32 + 4 * r : 96 : 16, :])
         plane_bytes = planes[:].bitcast(U8)

@@ -32,7 +32,7 @@ W4_AT = SLOTS + SLOT * (M_TILES - 1)
 SPARE = W4_AT + 6 + SLOT
 V_WORDS = PASSES * S // 4
 W4_WORDS = PASSES * M // 4
-GATE_AT = tuple(SLOTS + SLOT * i for i in (6, 7, 1, 2, 3, 0, 4, 5))
+GATE_AT = tuple(SLOTS + SLOT * i for i in (6, 7, 1, 2, 3, 5, 0, 4))
 GATE_AT = GATE_AT[:1] + (W4_AT + 6,) + GATE_AT[2:]
 STORE_GROUPS = ((0, 4, SPARE), (4, 7, SLOTS + SLOT), (7, 8, SLOTS + SLOT * 6))
 
@@ -117,7 +117,8 @@ def tile_list_tabgate_none_kernel(
 
         up_codes = keep.tile([P, M], U32, name="up_codes", align_bytes=64)
         up_plane = keep.tile([P, M], U8, name="up_plane", align_bytes=64)
-        for half in range(2):
+
+        def make_up(half):
             cols = slice(512 * half, 512 * (half + 1))
             grouped = placed([P, 512 * PACK], BF16, "up_grouped%d" % half, SLOTS + SLOT * 4 + 4 * half)
             nc.scalar.copy(
@@ -131,23 +132,24 @@ def tile_list_tabgate_none_kernel(
 
         def make_h(c, banks):
             grouped = placed([P, CHUNK * PACK], BF16, "h_grouped%d" % c, SLOTS + SLOT * 5 + 4 * c)
-            for b in range(CHUNK // H_COLS):
-                first = CHUNK * c + H_COLS * b
-                bank = psum.tile([P, PACK, H_COLS], F32, name="h_bank", offset=BANK * banks[b])
-                for t in range(PACK):
-                    for a in range(PASSES):
+            sums = [psum.tile([P, PACK, H_COLS], F32, name="h_bank", offset=BANK * b) for b in banks]
+            for a in range(PASSES):
+                for b in range(CHUNK // H_COLS):
+                    first = CHUNK * c + H_COLS * b
+                    for t in range(PACK):
                         nc.tensor.matmul_mx(
-                            out=bank[:, t, :],
+                            out=sums[b][:, t, :],
                             lhsT=down_codes[:, a, P * t : P * (t + 1)].bitcast(FP8X4),
                             lhsT_scale=down_plane[:, a, P * t : P * (t + 1)],
                             rhs=v_codes[:, a, first : first + H_COLS].bitcast(FP8X4),
                             rhs_scale=v_plane[a][:, first : first + H_COLS],
-                            start=(a == 0),
-                            stop=(a == PASSES - 1),
+                            start=(a == 0 and t == 0),
+                            stop=(a == PASSES - 1 and t == PACK - 1),
                         )
+            for b in range(CHUNK // H_COLS):
                 nc.scalar.copy(
                     out=grouped[:, H_COLS * PACK * b : H_COLS * PACK * (b + 1)].rearrange("p (n t) -> p n t", t=PACK),
-                    in_=bank[:].rearrange("p t n -> p n t"),
+                    in_=sums[b][:].rearrange("p t n -> p n t"),
                 )
             cols = slice(CHUNK * c, CHUNK * (c + 1))
             nc.vector.quantize_mx(out=h_codes[:, cols].bitcast(FP8X4), scales=h_plane[:, cols], in_=grouped[:])
@@ -194,22 +196,23 @@ def tile_list_tabgate_none_kernel(
 
         make_h(0, (0, 1, 2, 3))
         make_h(1, (4, 5, 6, 7))
-        for m in range(M_TILES - 1):
+        make_up(0)
+        make_h(2, (0, 1, 2, 3))
+        for m in range(M_TILES - 2):
             load_gates(m)
         out_rows = out.rearrange("(m p) s -> p m s", p=P)
         first, last, kib = STORE_GROUPS[0]
         result = placed([P, last - first, S], F32, "result0", kib)
         early = [ring.tile([P, S], F32, name="y_sb") for m in range(2)]
-        for c in range(2):
-            make_y(0, c, early[0], c)
-            gate(result[:, 0, :], 0, early[0], c, c + 1)
-        make_h(2, (0, 1, 0, 1))
-        load_gates(M_TILES - 1)
-        for c in range(2):
-            make_y(1, c, early[1], 2 + c)
-            gate(result[:, 1, :], 1, early[1], c, c + 1)
         for m in range(2):
-            make_y(m, 2, early[m], 4 + m)
+            for c in range(2):
+                make_y(m, c, early[m], 4 + 2 * m + c)
+                gate(result[:, m, :], m, early[m], c, c + 1)
+        make_up(1)
+        for m in range(M_TILES - 2, M_TILES):
+            load_gates(m)
+        for m in range(2):
+            make_y(m, 2, early[m], m)
             gate(result[:, m, :], m, early[m], 2, 3)
         for first, last, kib in STORE_GROUPS:
             if first > 0:
@@ -217,6 +220,6 @@ def tile_list_tabgate_none_kernel(
             for m in range(max(first, 2), last):
                 y_sb = ring.tile([P, S], F32, name="y_sb")
                 for c in range(CHUNKS):
-                    make_y(m, c, y_sb, (CHUNKS * m + c) % BANKS)
-                gate(result[:, m - first, :], m, y_sb, 0, CHUNKS)
+                    make_y(m, c, y_sb, (CHUNKS * m + c + 4) % BANKS)
+                    gate(result[:, m - first, :], m, y_sb, c, c + 1)
             nc.sync.dma_start(out=out_rows[:, first:last, :], in_=result[:])

@@ -28,13 +28,15 @@ BANK = 2048
 BANKS = 8
 SLOT = 16
 SLOTS = 20
-W4_AT = SLOTS + SLOT * (M_TILES - 1)
-SPARE = W4_AT + 6 + SLOT
+SPARE = SLOTS + SLOT * M_TILES
+W4_AT = SPARE + 24
 V_WORDS = PASSES * S // 4
 W4_WORDS = PASSES * M // 4
-GATE_AT = tuple(SLOTS + SLOT * i for i in (6, 7, 1, 2, 3, 5, 0, 4))
-GATE_AT = GATE_AT[:1] + (W4_AT + 6,) + GATE_AT[2:]
-STORE_GROUPS = ((0, 4, SPARE), (4, 7, SLOTS + SLOT), (7, 8, SLOTS + SLOT * 6))
+GATE_AT = tuple(SLOTS + SLOT * i for i in (6, 3, 0, 5, 7, 1, 4, 2))
+STORE_GROUPS = ((0, 4, SPARE), (4, 7, SLOTS + SLOT * 6 - 2), (7, 8, SLOTS))
+DOWN_GROUPED_AT = (SLOTS + SLOT * 4, W4_AT, SLOTS + SLOT * 6)
+H_GROUPED_AT = (SLOTS + SLOT * 5, SLOTS + SLOT * 7, SLOTS + SLOT)
+UP_GROUPED_AT = (SLOTS + SLOT * 7 + 4, SLOTS + SLOT * 2)
 
 
 def tile_list_tabgate_none_kernel(
@@ -47,19 +49,19 @@ def tile_list_tabgate_none_kernel(
         ring = ctx.enter_context(tc.tile_pool(name="ring", bufs=4))
         psum = ctx.enter_context(tc.psum_pool(name="psum", bufs=1))
 
-        def placed(shape, dtype, name, kib):
-            return arena.tile(shape, dtype, name=name, offset=int(1024 * kib), align_bytes=64)
+        def placed(shape, dtype, name, kib, align=64):
+            return arena.tile(shape, dtype, name=name, offset=int(1024 * kib), align_bytes=align)
 
         down_rows = down.rearrange("(a p j) r -> p a j r", p=P, j=PACK)
-        down_first = placed([P, PACK, R], F32, "down_first", SLOTS + SLOT)
+        down_first = placed([P, PACK, R], F32, "down_first", SLOTS)
         nc.sync.dma_start(out=down_first[:], in_=down_rows[:, 0, :, :])
         offsets = keep.tile([P, S // 16], U16, name="offsets")
         nc.sync.dma_start(offsets[:], offs)
-        down_rest = placed([P, PASSES - 1, PACK, R], F32, "down_rest", SPARE + 12)
+        down_rest = placed([P, PASSES - 1, PACK, R], F32, "down_rest", SLOTS + SLOT * 7)
         nc.sync.dma_start(out=down_rest[:], in_=down_rows[:, 1:PASSES, :, :])
         down_raw = [down_first[:], down_rest[:, 0, :, :], down_rest[:, 1, :, :]]
 
-        staged = placed([P, V_WORDS + W4_WORDS], I32, "staged", W4_AT - 0.75)
+        staged = placed([P, V_WORDS + W4_WORDS], I32, "staged", SLOTS + SLOT * 3)
         nc.sync.dma_start(
             out=staged[32:96:4, V_WORDS:].rearrange("q (a t) -> q a t", a=PASSES),
             in_=w4_scales.bitcast(I32).rearrange("a q t -> q a t"),
@@ -74,17 +76,17 @@ def tile_list_tabgate_none_kernel(
 
         down_grouped = []
         for a in range(PASSES):
-            grouped = placed([P, R * PACK], BF16, "down_grouped%d" % a, SLOTS + 4 if a == 0 else SLOTS + SLOT * 5 + 4 * a)
+            grouped = placed([P, R * PACK], BF16, "down_grouped%d" % a, DOWN_GROUPED_AT[a])
             nc.scalar.copy(
                 out=grouped[:].rearrange("p (t m j) -> p m j t", t=PACK, j=PACK),
                 in_=down_raw[a].rearrange("p j (m t) -> p m j t", t=PACK),
             )
             down_grouped.append(grouped)
 
-        words = placed([P, PASSES, T], I32, "words", SLOTS + SLOT)
+        words = placed([P, PASSES, T], I32, "words", SLOTS)
         nc.sync.dma_start(out=words[:], in_=tab_words.rearrange("a p t i -> p a (t i)").bitcast(I32))
 
-        picked = placed([P, PASSES, S], U8, "picked", 17.5)
+        picked = placed([P, PASSES, S], U8, "picked", 15)
         for a in range(PASSES):
             nc.vector.tensor_copy(picked[:, a, :], scale_window[:, a, :].bitcast(U8).indirect(offsets[:]))
             nc.vector.tensor_copy(out=staged[:, S // 4 * a : S // 4 * (a + 1)], in_=picked[:, a, :].bitcast(I32))
@@ -100,14 +102,14 @@ def tile_list_tabgate_none_kernel(
             nc.vector.quantize_mx(
                 out=down_codes[:, a, :].bitcast(FP8X4), scales=down_plane[:, a, :], in_=down_grouped[a][:]
             )
-        up_raw = placed([P, PACK, M], F32, "up_raw", SLOTS)
+        up_raw = placed([P, PACK, M], F32, "up_raw", SLOTS + SLOT * 4)
         nc.sync.dma_start(out=up_raw[:], in_=up.rearrange("(p j) n -> p j n", j=PACK))
         w4_codes = placed([P, PASSES, 2 * M], U8, "w4_codes", W4_AT)
         nc.sync.dma_start(
             out=w4_codes[:].bitcast(I32), in_=w4_words.bitcast(I32).rearrange("a p b -> p a b")
         )
 
-        v_codes = placed([P, PASSES, S], U32, "v_codes", 0)
+        v_codes = placed([P, PASSES, S], U32, "v_codes", 0, 4096)
         for c in range(CHUNKS):
             for a in range(PASSES):
                 nc.vector.tensor_copy(
@@ -120,7 +122,7 @@ def tile_list_tabgate_none_kernel(
 
         def make_up(half):
             cols = slice(512 * half, 512 * (half + 1))
-            grouped = placed([P, 512 * PACK], BF16, "up_grouped%d" % half, SLOTS + SLOT * 4 + 4 * half)
+            grouped = placed([P, 512 * PACK], BF16, "up_grouped%d" % half, UP_GROUPED_AT[half])
             nc.scalar.copy(
                 out=grouped[:].rearrange("p (c i j) -> p c j i", i=4, j=PACK),
                 in_=up_raw[:, :, cols].rearrange("p j (c i) -> p c j i", i=4),
@@ -131,7 +133,7 @@ def tile_list_tabgate_none_kernel(
         h_plane = keep.tile([P, S], U8, name="h_plane", align_bytes=64)
 
         def make_h(c, banks):
-            grouped = placed([P, CHUNK * PACK], BF16, "h_grouped%d" % c, SLOTS + SLOT * 5 + 4 * c)
+            grouped = placed([P, CHUNK * PACK], BF16, "h_grouped%d" % c, H_GROUPED_AT[c])
             sums = [psum.tile([P, PACK, H_COLS], F32, name="h_bank", offset=BANK * b) for b in banks]
             for a in range(PASSES):
                 for b in range(CHUNK // H_COLS):

@@ -34,7 +34,8 @@ V_WORDS = PASSES * S // 4
 W4_WORDS = PASSES * M // 4
 GATE_AT = tuple(SLOTS + SLOT * i for i in (6, 3, 0, 5, 7, 1, 4, 2))
 STORE_GROUPS = ((0, 4, SPARE), (4, 7, SLOTS + SLOT * 6 - 2), (7, 8, SLOTS))
-DOWN_GROUPED_AT = (SLOTS + SLOT * 4, W4_AT, SLOTS + SLOT * 6)
+DOWN_GROUPED_AT = (W4_AT, SLOTS + SLOT * 6, SLOTS + SLOT * 3 + 8)
+PICKED_AT = (16.5, 18, SLOTS + SLOT * 4)
 H_GROUPED_AT = (SLOTS + SLOT * 5, SLOTS + SLOT * 7, SLOTS + SLOT)
 UP_GROUPED_AT = (SLOTS + SLOT * 7 + 4, SLOTS + SLOT * 2)
 
@@ -86,10 +87,10 @@ def tile_list_tabgate_none_kernel(
         words = placed([P, PASSES, T], I32, "words", SLOTS)
         nc.sync.dma_start(out=words[:], in_=tab_words.rearrange("a p t i -> p a (t i)").bitcast(I32))
 
-        picked = placed([P, PASSES, S], U8, "picked", 15)
         for a in range(PASSES):
-            nc.vector.tensor_copy(picked[:, a, :], scale_window[:, a, :].bitcast(U8).indirect(offsets[:]))
-            nc.vector.tensor_copy(out=staged[:, S // 4 * a : S // 4 * (a + 1)], in_=picked[:, a, :].bitcast(I32))
+            picked = placed([P, S], U8, "picked%d" % a, PICKED_AT[a])
+            nc.vector.tensor_copy(picked[:], scale_window[:, a, :].bitcast(U8).indirect(offsets[:]))
+            nc.vector.tensor_copy(out=staged[:, S // 4 * a : S // 4 * (a + 1)], in_=picked[:].bitcast(I32))
         for r in range(4):
             nc.sync.dma_start(out=planes[r:P:32, :], in_=staged[32 + 4 * r : 96 : 16, :])
         plane_bytes = planes[:].bitcast(U8)

@@ -33,8 +33,9 @@ W4_AT = SPARE + 24
 V_WORDS = PASSES * S // 4
 W4_WORDS = PASSES * M // 4
 GATE_AT = tuple(SLOTS + SLOT * i for i in (6, 3, 0, 5, 7, 1, 4, 2))
-STORE_GROUPS = ((0, 4, SPARE), (4, 7, SLOTS + SLOT * 6 - 2), (7, 8, SLOTS))
-DOWN_GROUPED_AT = (W4_AT, SLOTS + SLOT * 6, SLOTS + SLOT * 3 + 8)
+STORE_GROUPS = ((0, 4, SPARE), (4, 7, SLOTS + SLOT * 6 - 4), (7, 8, SLOTS))
+W4_RAW_AT = SPARE + 12
+DOWN_GROUPED_AT = (W4_RAW_AT, SLOTS + SLOT * 6, SLOTS + SLOT * 3 + 8)
 PICKED_AT = (16.5, 18, SLOTS + SLOT * 4)
 H_GROUPED_AT = (SLOTS + SLOT * 5, SLOTS + SLOT * 7, SLOTS + SLOT)
 UP_GROUPED_AT = (SLOTS + SLOT * 7 + 4, SLOTS + SLOT * 2)
@@ -48,6 +49,7 @@ def tile_list_tabgate_none_kernel(
         keep = ctx.enter_context(tc.tile_pool(name="keep", bufs=1))
         arena = ctx.enter_context(tc.tile_pool(name="arena", bufs=1))
         ring = ctx.enter_context(tc.tile_pool(name="ring", bufs=4))
+        top = ctx.enter_context(tc.tile_pool(name="top", bufs=1))
         psum = ctx.enter_context(tc.psum_pool(name="psum", bufs=1))
 
         def placed(shape, dtype, name, kib, align=64):
@@ -95,7 +97,7 @@ def tile_list_tabgate_none_kernel(
             nc.sync.dma_start(out=planes[r:P:32, :], in_=staged[32 + 4 * r : 96 : 16, :])
         plane_bytes = planes[:].bitcast(U8)
         v_plane = [plane_bytes[:, S * a : S * (a + 1)] for a in range(PASSES)]
-        w4_plane = [plane_bytes[:, PASSES * S + M * a : PASSES * S + M * (a + 1)] for a in range(PASSES)]
+        w4_plane_raw = plane_bytes[:, PASSES * S :].rearrange("p (a n) -> p a n", a=PASSES)
 
         down_codes = keep.tile([P, PASSES, R], U32, name="down_codes", align_bytes=64)
         down_plane = placed([P, PASSES, R], U8, "down_plane", 18)
@@ -105,10 +107,23 @@ def tile_list_tabgate_none_kernel(
             )
         up_raw = placed([P, PACK, M], F32, "up_raw", SLOTS + SLOT * 4)
         nc.sync.dma_start(out=up_raw[:], in_=up.rearrange("(p j) n -> p j n", j=PACK))
-        w4_codes = placed([P, PASSES, 2 * M], U8, "w4_codes", W4_AT)
+        w4_raw = placed([P, PASSES, 2 * M], U8, "w4_raw", W4_RAW_AT)
         nc.sync.dma_start(
-            out=w4_codes[:].bitcast(I32), in_=w4_words.bitcast(I32).rearrange("a p b -> p a b")
+            out=w4_raw[:].bitcast(I32), in_=w4_words.bitcast(I32).rearrange("a p b -> p a b")
         )
+        w4_codes = placed([P, PASSES, 2 * M], U8, "w4_codes", W4_AT)
+        w4_plane = top.tile([P, PASSES, M], U8, name="w4_plane", align_bytes=64)
+
+        def deal_w4(half):
+            cols = slice(512 * half, 512 * (half + 1))
+            nc.vector.tensor_copy(
+                out=w4_plane[:, :, cols].rearrange("p a (e q) -> p a e q", e=PACK),
+                in_=w4_plane_raw[:, :, cols].rearrange("p a (q e) -> p a e q", e=PACK),
+            )
+            nc.vector.tensor_copy(
+                out=w4_codes[:].bitcast(U16)[:, :, cols].rearrange("p a (e q) -> p a e q", e=PACK),
+                in_=w4_raw[:].bitcast(U16)[:, :, cols].rearrange("p a (q e) -> p a e q", e=PACK),
+            )
 
         v_codes = placed([P, PASSES, S], U32, "v_codes", 0, 4096)
         for c in range(CHUNKS):
@@ -125,8 +140,8 @@ def tile_list_tabgate_none_kernel(
             cols = slice(512 * half, 512 * (half + 1))
             grouped = placed([P, 512 * PACK], BF16, "up_grouped%d" % half, UP_GROUPED_AT[half])
             nc.scalar.copy(
-                out=grouped[:].rearrange("p (c i j) -> p c j i", i=4, j=PACK),
-                in_=up_raw[:, :, cols].rearrange("p j (c i) -> p c j i", i=4),
+                out=grouped[:].rearrange("p (e q j) -> p q j e", e=PACK, j=PACK),
+                in_=up_raw[:, :, cols].rearrange("p j (q e) -> p q j e", e=PACK),
             )
             nc.vector.quantize_mx(out=up_codes[:, cols].bitcast(FP8X4), scales=up_plane[:, cols], in_=grouped[:])
 
@@ -164,7 +179,7 @@ def tile_list_tabgate_none_kernel(
                 nc.tensor.matmul_mx(
                     out=acc[:],
                     lhsT=w4_codes[:, a, 2 * P * m : 2 * P * (m + 1)].bitcast(FP4X4),
-                    lhsT_scale=w4_plane[a][:, P * m : P * (m + 1)],
+                    lhsT_scale=w4_plane[:, a, P * m : P * (m + 1)],
                     rhs=v_codes[:, a, cols].bitcast(FP8X4),
                     rhs_scale=v_plane[a][:, cols],
                     start=(a == 0),
@@ -182,10 +197,11 @@ def tile_list_tabgate_none_kernel(
             nc.scalar.copy(out=y_sb[:, cols], in_=acc[:])
 
         gates = []
+        gate_dealt = gT.rearrange("(g p e) t -> g e p t", p=P, e=PACK)
 
         def load_gates(m):
             gate_rows = placed([P, T], F32, "gates%d" % m, GATE_AT[m])
-            nc.sync.dma_start(out=gate_rows[:], in_=gT[P * m : P * (m + 1), :])
+            nc.sync.dma_start(out=gate_rows[:], in_=gate_dealt[m // PACK, m % PACK])
             gates.append(gate_rows)
 
         def gate(result, m, y_sb, first, last):
@@ -200,10 +216,12 @@ def tile_list_tabgate_none_kernel(
         make_h(0, (0, 1, 2, 3))
         make_h(1, (4, 5, 6, 7))
         make_up(0)
+        deal_w4(0)
+        deal_w4(1)
         make_h(2, (0, 1, 2, 3))
         for m in range(M_TILES - 2):
             load_gates(m)
-        out_rows = out.rearrange("(m p) s -> p m s", p=P)
+        out_rows = out.rearrange("(g p e) s -> g p (e s)", p=P, e=PACK)
         first, last, kib = STORE_GROUPS[0]
         result = placed([P, last - first, S], F32, "result0", kib)
         early = [ring.tile([P, S], F32, name="y_sb") for m in range(2)]
@@ -217,6 +235,9 @@ def tile_list_tabgate_none_kernel(
         for m in range(2):
             make_y(m, 2, early[m], m)
             gate(result[:, m, :], m, early[m], 2, 3)
+        nc.scalar.dma_start(
+            out=out_rows[0, :, 0 : 2 * S], in_=result[:, 0:2, :].rearrange("p m s -> p (m s)")
+        )
         for first, last, kib in STORE_GROUPS:
             if first > 0:
                 result = placed([P, last - first, S], F32, "result%d" % first, kib)
@@ -225,4 +246,7 @@ def tile_list_tabgate_none_kernel(
                 for c in range(CHUNKS):
                     make_y(m, c, y_sb, (CHUNKS * m + c + 4) % BANKS)
                     gate(result[:, m - first, :], m, y_sb, c, c + 1)
-            nc.sync.dma_start(out=out_rows[:, first:last, :], in_=result[:])
+            nc.sync.dma_start(
+                out=out_rows[first // PACK, :, S * (max(first, 2) % PACK) : S * (first % PACK + last - first)],
+                in_=result[:, max(first, 2) - first :, :].rearrange("p m s -> p (m s)"),
+            )

@@ -71,7 +71,7 @@ def tile_list_tabgate_none_kernel(
         )
         scale_window = placed([P, PASSES, T // 4], I32, "scale_window", SPARE)
         nc.vector.memset(scale_window[:], 0)
-        nc.sync.dma_start(
+        nc.scalar.dma_start(
             out=scale_window[32:96:4, :, :], in_=tab_scales.bitcast(I32).rearrange("a q t -> q a t")
         )
         planes = keep.tile([P, V_WORDS + W4_WORDS], I32, name="planes", align_bytes=64)
@@ -80,7 +80,8 @@ def tile_list_tabgate_none_kernel(
         down_grouped = []
         for a in range(PASSES):
             grouped = placed([P, R * PACK], BF16, "down_grouped%d" % a, DOWN_GROUPED_AT[a])
-            nc.scalar.copy(
+            interleave = nc.vector.tensor_copy if a == 0 else nc.scalar.copy
+            interleave(
                 out=grouped[:].rearrange("p (t m j) -> p m j t", t=PACK, j=PACK),
                 in_=down_raw[a].rearrange("p j (m t) -> p m j t", t=PACK),
             )

@@ -32,13 +32,14 @@ SPARE = SLOTS + SLOT * M_TILES
 W4_AT = SPARE + 24
 V_WORDS = PASSES * S // 4
 W4_WORDS = PASSES * M // 4
-GATE_AT = tuple(SLOTS + SLOT * i for i in (6, 3, 0, 5, 7, 1, 4, 2))
+GATE_AT = tuple(SLOTS + SLOT * i for i in (6, 3, 0, 5, 7, 4, 1, 2))
 STORE_GROUPS = ((0, 4, SPARE), (4, 7, SLOTS + SLOT * 6 - 4), (7, 8, SLOTS))
 W4_RAW_AT = SPARE + 12
 DOWN_GROUPED_AT = (W4_RAW_AT, SLOTS + SLOT * 6, SLOTS + SLOT * 3 + 8)
-PICKED_AT = (16.5, 18, SLOTS + SLOT * 4)
-H_GROUPED_AT = (SLOTS + SLOT * 5, SLOTS + SLOT * 7, SLOTS + SLOT)
-UP_GROUPED_AT = (SLOTS + SLOT * 7 + 4, SLOTS + SLOT * 2)
+H_GROUPED_AT = (SLOTS + SLOT * 5, SLOTS + SLOT * 7, SLOTS + SLOT * 2 - 2)
+UP_PARTS = 4
+UP_COLS = M // UP_PARTS
+UP_GROUPED_AT = (SLOTS + SLOT * 7 + 4,) + (H_GROUPED_AT[2] + 1,) * (UP_PARTS - 1)
 
 
 def tile_list_tabgate_none_kernel(
@@ -64,18 +65,18 @@ def tile_list_tabgate_none_kernel(
         nc.sync.dma_start(out=down_rest[:], in_=down_rows[:, 1:PASSES, :, :])
         down_raw = [down_first[:], down_rest[:, 0, :, :], down_rest[:, 1, :, :]]
 
-        staged = placed([P, V_WORDS + W4_WORDS], I32, "staged", SLOTS + SLOT * 3)
-        nc.sync.dma_start(
-            out=staged[32:96:4, V_WORDS:].rearrange("q (a t) -> q a t", a=PASSES),
-            in_=w4_scales.bitcast(I32).rearrange("a q t -> q a t"),
-        )
-        scale_window = placed([P, PASSES, T // 4], I32, "scale_window", SPARE)
+        scale_window = placed([P, PASSES, T // 4], I32, "scale_window", SLOTS + SLOT * 4)
         nc.vector.memset(scale_window[:], 0)
         nc.scalar.dma_start(
             out=scale_window[32:96:4, :, :], in_=tab_scales.bitcast(I32).rearrange("a q t -> q a t")
         )
         planes = keep.tile([P, V_WORDS + W4_WORDS], I32, name="planes", align_bytes=64)
         nc.vector.memset(planes[:], 0)
+        w4_scale_rows = w4_scales.bitcast(I32).rearrange("a (g r) t -> r g a t", r=4)
+        for r in range(4):
+            nc.sync.dma_start(
+                out=planes[r:P:32, V_WORDS:].rearrange("g (a t) -> g a t", a=PASSES), in_=w4_scale_rows[r]
+            )
 
         down_grouped = []
         for a in range(PASSES):
@@ -90,12 +91,13 @@ def tile_list_tabgate_none_kernel(
         words = placed([P, PASSES, T], I32, "words", SLOTS)
         nc.sync.dma_start(out=words[:], in_=tab_words.rearrange("a p t i -> p a (t i)").bitcast(I32))
 
+        picked = placed([P, PASSES * S], U8, "picked", SLOTS + SLOT * 3)
         for a in range(PASSES):
-            picked = placed([P, S], U8, "picked%d" % a, PICKED_AT[a])
-            nc.vector.tensor_copy(picked[:], scale_window[:, a, :].bitcast(U8).indirect(offsets[:]))
-            nc.vector.tensor_copy(out=staged[:, S // 4 * a : S // 4 * (a + 1)], in_=picked[:].bitcast(I32))
+            nc.vector.tensor_copy(
+                picked[:, S * a : S * (a + 1)], scale_window[:, a, :].bitcast(U8).indirect(offsets[:])
+            )
         for r in range(4):
-            nc.sync.dma_start(out=planes[r:P:32, :], in_=staged[32 + 4 * r : 96 : 16, :])
+            nc.sync.dma_start(out=planes[r:P:32, 0:V_WORDS], in_=picked[32 + 4 * r : 96 : 16, :].bitcast(I32))
         plane_bytes = planes[:].bitcast(U8)
         v_plane = [plane_bytes[:, S * a : S * (a + 1)] for a in range(PASSES)]
         w4_plane_raw = plane_bytes[:, PASSES * S :].rearrange("p (a n) -> p a n", a=PASSES)
@@ -137,12 +139,14 @@ def tile_list_tabgate_none_kernel(
         up_codes = keep.tile([P, M], U32, name="up_codes", align_bytes=64)
         up_plane = keep.tile([P, M], U8, name="up_plane", align_bytes=64)
 
-        def make_up(half):
-            cols = slice(512 * half, 512 * (half + 1))
-            grouped = placed([P, 512 * PACK], BF16, "up_grouped%d" % half, UP_GROUPED_AT[half])
+        up_dealt = up_raw[:].rearrange("p j (g q u e) -> p g u q j e", g=2, u=2, e=2)
+
+        def make_up(part):
+            cols = slice(UP_COLS * part, UP_COLS * (part + 1))
+            grouped = placed([P, UP_COLS * PACK], BF16, "up_grouped%d" % part, UP_GROUPED_AT[part])
             nc.scalar.copy(
-                out=grouped[:].rearrange("p (e q j) -> p q j e", e=PACK, j=PACK),
-                in_=up_raw[:, :, cols].rearrange("p j (q e) -> p q j e", e=PACK),
+                out=grouped[:].rearrange("p (e q j) -> p q j e", e=2, j=PACK),
+                in_=up_dealt[:, part // 2, part % 2],
             )
             nc.vector.quantize_mx(out=up_codes[:, cols].bitcast(FP8X4), scales=up_plane[:, cols], in_=grouped[:])
 
@@ -214,13 +218,13 @@ def tile_list_tabgate_none_kernel(
                 MULT,
             )
 
+        make_up(0)
         make_h(0, (0, 1, 2, 3))
         make_h(1, (4, 5, 6, 7))
-        make_up(0)
         deal_w4(0)
         deal_w4(1)
         make_h(2, (0, 1, 2, 3))
-        for m in range(M_TILES - 2):
+        for m in range(M_TILES - 3):
             load_gates(m)
         out_rows = out.rearrange("(g p e) s -> g p (e s)", p=P, e=PACK)
         first, last, kib = STORE_GROUPS[0]
@@ -230,8 +234,9 @@ def tile_list_tabgate_none_kernel(
             for c in range(2):
                 make_y(m, c, early[m], 4 + 2 * m + c)
                 gate(result[:, m, :], m, early[m], c, c + 1)
-        make_up(1)
-        for m in range(M_TILES - 2, M_TILES):
+        for part in range(1, UP_PARTS):
+            make_up(part)
+        for m in range(M_TILES - 3, M_TILES):
             load_gates(m)
         for m in range(2):
             make_y(m, 2, early[m], m)

@@ -33,7 +33,7 @@ W4_AT = SPARE + 24
 V_WORDS = PASSES * S // 4
 W4_WORDS = PASSES * M // 4
 GATE_AT = tuple(SLOTS + SLOT * i for i in (6, 3, 0, 5, 7, 4, 1, 2))
-STORE_GROUPS = ((0, 4, SPARE), (4, 7, SLOTS + SLOT * 6 - 4), (7, 8, SLOTS))
+STORE_GROUPS = ((0, 4, SPARE), (4, 6, SLOTS + SLOT * 6 - 4), (6, 7, SLOTS + SLOT * 6 + 8), (7, 8, SLOTS))
 W4_RAW_AT = SPARE + 12
 DOWN_GROUPED_AT = (W4_RAW_AT, SLOTS + SLOT * 6, SLOTS + SLOT * 3 + 8)
 H_GROUPED_AT = (SLOTS + SLOT * 5, SLOTS + SLOT * 7, SLOTS + SLOT * 2 - 2)

@@ -18,28 +18,35 @@ MULT = mybir.AluOpType.mult
 P = 128
 PACK = 4
 PASSES = K // (P * PACK)
+SCALE_ROWS = 16
 CHUNK = 512
 CHUNKS = S // CHUNK
 H_COLS = 128
 M_TILES = M // P
 LIST_COLS = CHUNK // 16
-
 BANK = 2048
 BANKS = 8
-SLOT = 16
-SLOTS = 20
-SPARE = SLOTS + SLOT * M_TILES
-W4_AT = SPARE + 24
-V_WORDS = PASSES * S // 4
-W4_WORDS = PASSES * M // 4
-GATE_AT = tuple(SLOTS + SLOT * i for i in (6, 3, 0, 5, 7, 4, 1, 2))
-STORE_GROUPS = ((0, 4, SPARE), (4, 6, SLOTS + SLOT * 6 - 4), (6, 7, SLOTS + SLOT * 6 + 8), (7, 8, SLOTS))
-W4_RAW_AT = SPARE + 12
-DOWN_GROUPED_AT = (W4_RAW_AT, SLOTS + SLOT * 6, SLOTS + SLOT * 3 + 8)
-H_GROUPED_AT = (SLOTS + SLOT * 5, SLOTS + SLOT * 7, SLOTS + SLOT * 2 - 2)
 UP_PARTS = 4
 UP_COLS = M // UP_PARTS
-UP_GROUPED_AT = (SLOTS + SLOT * 7 + 4,) + (H_GROUPED_AT[2] + 1,) * (UP_PARTS - 1)
+ROW_BYTES = S + M
+SPREAD_FIRST = 48
+SPREAD_STEP = 1
+
+SLOT = 16
+RESULTS_AT = SLOT * M_TILES
+TILE_KIB = 6
+STORE_GROUPS = ((0, 4), (4, 7), (7, 8))
+TABLE_AT = (2 * SLOT, 0, SLOT)
+WINDOW_AT = SLOT - 2
+DOWN_RAW_AT = RESULTS_AT
+DOWN_GROUPED_AT = (RESULTS_AT + 24, RESULTS_AT + 28, 4 * SLOT + 8)
+W4_RAW_AT = DOWN_GROUPED_AT[1]
+UP_RAW_AT = DOWN_GROUPED_AT[2]
+PICKED_AT = RESULTS_AT + 36
+STAGE_AT = RESULTS_AT + 40
+DOWN_CODES_AT = 3 * SLOT + 4
+H_GROUPED_AT = (2 * SLOT, 3 * SLOT, 7 * SLOT - 2)
+UP_GROUPED_AT = (6 * SLOT + 4,) + (7 * SLOT - 1,) * (UP_PARTS - 1)
 
 
 def tile_list_tabgate_none_kernel(
@@ -49,96 +56,92 @@ def tile_list_tabgate_none_kernel(
     with ExitStack() as ctx:
         keep = ctx.enter_context(tc.tile_pool(name="keep", bufs=1))
         arena = ctx.enter_context(tc.tile_pool(name="arena", bufs=1))
-        ring = ctx.enter_context(tc.tile_pool(name="ring", bufs=4))
-        top = ctx.enter_context(tc.tile_pool(name="top", bufs=1))
+        ring = ctx.enter_context(tc.tile_pool(name="ring", bufs=6))
         psum = ctx.enter_context(tc.psum_pool(name="psum", bufs=1))
 
         def placed(shape, dtype, name, kib, align=64):
-            return arena.tile(shape, dtype, name=name, offset=int(1024 * kib), align_bytes=align)
+            return arena.tile(shape, dtype, name=name, offset=1024 * kib, align_bytes=align)
 
         down_rows = down.rearrange("(a p j) r -> p a j r", p=P, j=PACK)
-        down_first = placed([P, PACK, R], F32, "down_first", SLOTS)
+        down_first = placed([P, PACK, R], F32, "down_first", DOWN_RAW_AT, 4096)
         nc.sync.dma_start(out=down_first[:], in_=down_rows[:, 0, :, :])
         offsets = keep.tile([P, S // 16], U16, name="offsets")
         nc.sync.dma_start(offsets[:], offs)
-        down_rest = placed([P, PASSES - 1, PACK, R], F32, "down_rest", SLOTS + SLOT * 7)
+
+        spread = slice(SPREAD_FIRST, SPREAD_FIRST + SPREAD_STEP * PASSES * SCALE_ROWS, SPREAD_STEP)
+        window = placed([P, T // 4], I32, "window", WINDOW_AT)
+        nc.vector.memset(window[0 : spread.start, :], 0)
+        nc.vector.memset(window[spread.stop : P, :], 0)
+        nc.sync.dma_start(out=window[spread, :], in_=tab_scales.bitcast(I32).rearrange("a q t -> (a q) t"))
+        stage = placed([P, ROW_BYTES // 4], I32, "stage", STAGE_AT)
+        nc.sync.dma_start(out=stage[spread, S // 4 :], in_=w4_scales.bitcast(I32).rearrange("a q n -> (a q) n"))
+        down_rest = placed([P, PASSES - 1, PACK, R], F32, "down_rest", DOWN_RAW_AT + 8)
         nc.sync.dma_start(out=down_rest[:], in_=down_rows[:, 1:PASSES, :, :])
         down_raw = [down_first[:], down_rest[:, 0, :, :], down_rest[:, 1, :, :]]
-
-        scale_window = placed([P, PASSES, T // 4], I32, "scale_window", SLOTS + SLOT * 4)
-        nc.vector.memset(scale_window[:], 0)
-        nc.scalar.dma_start(
-            out=scale_window[32:96:4, :, :], in_=tab_scales.bitcast(I32).rearrange("a q t -> q a t")
-        )
-        planes = keep.tile([P, V_WORDS + W4_WORDS], I32, name="planes", align_bytes=64)
+        planes = keep.tile([P, PASSES, ROW_BYTES // 4], I32, name="planes", align_bytes=64)
         nc.vector.memset(planes[:], 0)
-        w4_scale_rows = w4_scales.bitcast(I32).rearrange("a (g r) t -> r g a t", r=4)
-        for r in range(4):
-            nc.sync.dma_start(
-                out=planes[r:P:32, V_WORDS:].rearrange("g (a t) -> g a t", a=PASSES), in_=w4_scale_rows[r]
-            )
 
+        picked = placed([P, S], U8, "picked", PICKED_AT)
+        nc.vector.tensor_copy(picked[:], window[:].bitcast(U8).indirect(offsets[:]))
+        nc.vector.tensor_copy(out=stage[:, 0 : S // 4], in_=picked[:].bitcast(I32))
+
+        table = []
+        for a in range(PASSES):
+            words = placed([P, T], I32, "words%d" % a, TABLE_AT[a])
+            nc.sync.dma_start(out=words[:], in_=tab_words[a].rearrange("p t i -> p (t i)").bitcast(I32))
+            table.append(words)
+            for r in range(4):
+                first = SPREAD_FIRST + SPREAD_STEP * (SCALE_ROWS * a + r)
+                nc.sync.dma_start(
+                    out=planes[r:P:32, a, :], in_=stage[first : first + 16 * SPREAD_STEP : 4 * SPREAD_STEP, :]
+                )
+        plane_bytes = planes[:].bitcast(U8)
+
+        down_codes = placed([P, PASSES, R], U32, "down_codes", DOWN_CODES_AT)
+        down_plane = placed([P, PASSES, R], U8, "down_plane", DOWN_CODES_AT + 6)
         down_grouped = []
         for a in range(PASSES):
             grouped = placed([P, R * PACK], BF16, "down_grouped%d" % a, DOWN_GROUPED_AT[a])
-            interleave = nc.vector.tensor_copy if a == 0 else nc.scalar.copy
+            interleave = nc.vector.tensor_copy if a == 1 else nc.scalar.copy
             interleave(
                 out=grouped[:].rearrange("p (t m j) -> p m j t", t=PACK, j=PACK),
                 in_=down_raw[a].rearrange("p j (m t) -> p m j t", t=PACK),
             )
             down_grouped.append(grouped)
-
-        words = placed([P, PASSES, T], I32, "words", SLOTS)
-        nc.sync.dma_start(out=words[:], in_=tab_words.rearrange("a p t i -> p a (t i)").bitcast(I32))
-
-        picked = placed([P, PASSES * S], U8, "picked", SLOTS + SLOT * 3)
-        for a in range(PASSES):
-            nc.vector.tensor_copy(
-                picked[:, S * a : S * (a + 1)], scale_window[:, a, :].bitcast(U8).indirect(offsets[:])
-            )
-        for r in range(4):
-            nc.sync.dma_start(out=planes[r:P:32, 0:V_WORDS], in_=picked[32 + 4 * r : 96 : 16, :].bitcast(I32))
-        plane_bytes = planes[:].bitcast(U8)
-        v_plane = [plane_bytes[:, S * a : S * (a + 1)] for a in range(PASSES)]
-        w4_plane_raw = plane_bytes[:, PASSES * S :].rearrange("p (a n) -> p a n", a=PASSES)
-
-        down_codes = keep.tile([P, PASSES, R], U32, name="down_codes", align_bytes=64)
-        down_plane = placed([P, PASSES, R], U8, "down_plane", 18)
         for a in range(PASSES):
             nc.vector.quantize_mx(
                 out=down_codes[:, a, :].bitcast(FP8X4), scales=down_plane[:, a, :], in_=down_grouped[a][:]
             )
-        up_raw = placed([P, PACK, M], F32, "up_raw", SLOTS + SLOT * 4)
-        nc.sync.dma_start(out=up_raw[:], in_=up.rearrange("(p j) n -> p j n", j=PACK))
+
         w4_raw = placed([P, PASSES, 2 * M], U8, "w4_raw", W4_RAW_AT)
-        nc.sync.dma_start(
-            out=w4_raw[:].bitcast(I32), in_=w4_words.bitcast(I32).rearrange("a p b -> p a b")
-        )
-        w4_codes = placed([P, PASSES, 2 * M], U8, "w4_codes", W4_AT)
-        w4_plane = top.tile([P, PASSES, M], U8, name="w4_plane", align_bytes=64)
+        nc.sync.dma_start(out=w4_raw[:].bitcast(I32), in_=w4_words.bitcast(I32).rearrange("a p b -> p a b"))
+        up_raw = placed([P, PACK, M], F32, "up_raw", UP_RAW_AT)
+        nc.sync.dma_start(out=up_raw[:], in_=up.rearrange("(p j) n -> p j n", j=PACK))
+
+        v_codes = keep.tile([P, PASSES, S], U32, name="v_codes", align_bytes=64)
+        for a in range(PASSES):
+            for c in range(CHUNKS):
+                nc.vector.tensor_copy(
+                    v_codes[:, a, CHUNK * c : CHUNK * (c + 1)],
+                    table[a][:].bitcast(U32).indirect(offsets[:, LIST_COLS * c : LIST_COLS * (c + 1)]),
+                )
+
+        w4_codes = keep.tile([P, PASSES, 2 * M], U8, name="w4_codes", align_bytes=64)
+        w4_plane = keep.tile([P, PASSES, M], U8, name="w4_plane", align_bytes=64)
 
         def deal_w4(half):
             cols = slice(512 * half, 512 * (half + 1))
             nc.vector.tensor_copy(
                 out=w4_plane[:, :, cols].rearrange("p a (e q) -> p a e q", e=PACK),
-                in_=w4_plane_raw[:, :, cols].rearrange("p a (q e) -> p a e q", e=PACK),
+                in_=plane_bytes[:, :, S + 512 * half : S + 512 * (half + 1)].rearrange("p a (q e) -> p a e q", e=PACK),
             )
             nc.vector.tensor_copy(
                 out=w4_codes[:].bitcast(U16)[:, :, cols].rearrange("p a (e q) -> p a e q", e=PACK),
                 in_=w4_raw[:].bitcast(U16)[:, :, cols].rearrange("p a (q e) -> p a e q", e=PACK),
             )
 
-        v_codes = placed([P, PASSES, S], U32, "v_codes", 0, 4096)
-        for c in range(CHUNKS):
-            for a in range(PASSES):
-                nc.vector.tensor_copy(
-                    v_codes[:, a, CHUNK * c : CHUNK * (c + 1)],
-                    words[:, a, :].bitcast(U32).indirect(offsets[:, LIST_COLS * c : LIST_COLS * (c + 1)]),
-                )
-
         up_codes = keep.tile([P, M], U32, name="up_codes", align_bytes=64)
         up_plane = keep.tile([P, M], U8, name="up_plane", align_bytes=64)
-
         up_dealt = up_raw[:].rearrange("p j (g q u e) -> p g u q j e", g=2, u=2, e=2)
 
         def make_up(part):
@@ -153,22 +156,25 @@ def tile_list_tabgate_none_kernel(
         h_codes = keep.tile([P, S], U32, name="h_codes", align_bytes=64)
         h_plane = keep.tile([P, S], U8, name="h_plane", align_bytes=64)
 
-        def make_h(c, banks):
+        def h_banks(banks):
+            return [psum.tile([P, PACK, H_COLS], F32, name="h_bank", offset=BANK * b) for b in banks]
+
+        def h_pass(c, a, sums):
+            for b in range(CHUNK // H_COLS):
+                first = CHUNK * c + H_COLS * b
+                for t in range(PACK):
+                    nc.tensor.matmul_mx(
+                        out=sums[b][:, t, :],
+                        lhsT=down_codes[:, a, P * t : P * (t + 1)].bitcast(FP8X4),
+                        lhsT_scale=down_plane[:, a, P * t : P * (t + 1)],
+                        rhs=v_codes[:, a, first : first + H_COLS].bitcast(FP8X4),
+                        rhs_scale=plane_bytes[:, a, first : first + H_COLS],
+                        start=(a == 0 and t == 0),
+                        stop=(a == PASSES - 1 and t == PACK - 1),
+                    )
+
+        def finish_h(c, sums):
             grouped = placed([P, CHUNK * PACK], BF16, "h_grouped%d" % c, H_GROUPED_AT[c])
-            sums = [psum.tile([P, PACK, H_COLS], F32, name="h_bank", offset=BANK * b) for b in banks]
-            for a in range(PASSES):
-                for b in range(CHUNK // H_COLS):
-                    first = CHUNK * c + H_COLS * b
-                    for t in range(PACK):
-                        nc.tensor.matmul_mx(
-                            out=sums[b][:, t, :],
-                            lhsT=down_codes[:, a, P * t : P * (t + 1)].bitcast(FP8X4),
-                            lhsT_scale=down_plane[:, a, P * t : P * (t + 1)],
-                            rhs=v_codes[:, a, first : first + H_COLS].bitcast(FP8X4),
-                            rhs_scale=v_plane[a][:, first : first + H_COLS],
-                            start=(a == 0 and t == 0),
-                            stop=(a == PASSES - 1 and t == PACK - 1),
-                        )
             for b in range(CHUNK // H_COLS):
                 nc.scalar.copy(
                     out=grouped[:, H_COLS * PACK * b : H_COLS * PACK * (b + 1)].rearrange("p (n t) -> p n t", t=PACK),
@@ -177,7 +183,15 @@ def tile_list_tabgate_none_kernel(
             cols = slice(CHUNK * c, CHUNK * (c + 1))
             nc.vector.quantize_mx(out=h_codes[:, cols].bitcast(FP8X4), scales=h_plane[:, cols], in_=grouped[:])
 
-        def make_y(m, c, y_sb, bank):
+        gates = []
+        gate_dealt = gT.rearrange("(g p e) t -> g e p t", p=P, e=PACK)
+
+        def load_gates(m):
+            gate_rows = placed([P, T], F32, "gates%d" % m, SLOT * m)
+            nc.sync.dma_start(out=gate_rows[:], in_=gate_dealt[m // PACK, m % PACK])
+            gates.append(gate_rows)
+
+        def make_out(m, c, result, bank):
             cols = slice(CHUNK * c, CHUNK * (c + 1))
             acc = psum.tile([P, CHUNK], F32, name="y_bank", offset=BANK * bank)
             for a in range(PASSES):
@@ -186,7 +200,7 @@ def tile_list_tabgate_none_kernel(
                     lhsT=w4_codes[:, a, 2 * P * m : 2 * P * (m + 1)].bitcast(FP4X4),
                     lhsT_scale=w4_plane[:, a, P * m : P * (m + 1)],
                     rhs=v_codes[:, a, cols].bitcast(FP8X4),
-                    rhs_scale=v_plane[a][:, cols],
+                    rhs_scale=plane_bytes[:, a, cols],
                     start=(a == 0),
                     stop=False,
                 )
@@ -199,60 +213,46 @@ def tile_list_tabgate_none_kernel(
                 start=False,
                 stop=True,
             )
-            nc.scalar.copy(out=y_sb[:, cols], in_=acc[:])
-
-        gates = []
-        gate_dealt = gT.rearrange("(g p e) t -> g e p t", p=P, e=PACK)
-
-        def load_gates(m):
-            gate_rows = placed([P, T], F32, "gates%d" % m, GATE_AT[m])
-            nc.sync.dma_start(out=gate_rows[:], in_=gate_dealt[m // PACK, m % PACK])
-            gates.append(gate_rows)
-
-        def gate(result, m, y_sb, first, last):
-            cols = slice(CHUNK * first, CHUNK * last)
+            y_sb = ring.tile([P, CHUNK], F32, name="y_sb")
+            nc.scalar.copy(out=y_sb[:], in_=acc[:])
             nc.vector.tensor_tensor(
-                result[:, cols],
-                gates[m][:].indirect(offsets[:, LIST_COLS * first : LIST_COLS * last]),
-                y_sb[:, cols],
-                MULT,
+                result[:, cols], gates[m][:].indirect(offsets[:, LIST_COLS * c : LIST_COLS * (c + 1)]), y_sb[:], MULT
             )
 
-        make_up(0)
-        make_h(0, (0, 1, 2, 3))
-        make_h(1, (4, 5, 6, 7))
-        deal_w4(0)
-        deal_w4(1)
-        make_h(2, (0, 1, 2, 3))
-        for m in range(M_TILES - 3):
-            load_gates(m)
-        out_rows = out.rearrange("(g p e) s -> g p (e s)", p=P, e=PACK)
-        first, last, kib = STORE_GROUPS[0]
-        result = placed([P, last - first, S], F32, "result0", kib)
-        early = [ring.tile([P, S], F32, name="y_sb") for m in range(2)]
-        for m in range(2):
+        first_sums = [h_banks((0, 1, 2, 3)), h_banks((4, 5, 6, 7))]
+        for a in range(PASSES):
             for c in range(2):
-                make_y(m, c, early[m], 4 + 2 * m + c)
-                gate(result[:, m, :], m, early[m], c, c + 1)
+                h_pass(c, a, first_sums[c])
+        finish_h(0, first_sums[0])
+        deal_w4(0)
+        finish_h(1, first_sums[1])
+        last_sums = h_banks((0, 1, 2, 3))
+        for a in range(PASSES):
+            h_pass(2, a, last_sums)
+        make_up(0)
+        for m in range(4):
+            load_gates(m)
+        results = [
+            placed([P, last - first, S], F32, "result%d" % first, RESULTS_AT + TILE_KIB * first)
+            for first, last in STORE_GROUPS
+        ]
+        for c in range(2):
+            make_out(0, c, results[0][:, 0, :], 4 + c)
+        finish_h(2, last_sums)
+        make_out(0, 2, results[0][:, 0, :], 6)
         for part in range(1, UP_PARTS):
             make_up(part)
-        for m in range(M_TILES - 3, M_TILES):
+        for m in range(4, M_TILES):
             load_gates(m)
-        for m in range(2):
-            make_y(m, 2, early[m], m)
-            gate(result[:, m, :], m, early[m], 2, 3)
-        nc.scalar.dma_start(
-            out=out_rows[0, :, 0 : 2 * S], in_=result[:, 0:2, :].rearrange("p m s -> p (m s)")
-        )
-        for first, last, kib in STORE_GROUPS:
-            if first > 0:
-                result = placed([P, last - first, S], F32, "result%d" % first, kib)
-            for m in range(max(first, 2), last):
-                y_sb = ring.tile([P, S], F32, name="y_sb")
+
+        out_rows = out.rearrange("(g p e) s -> g p (e s)", p=P, e=PACK)
+        for (first, last), result in zip(STORE_GROUPS, results):
+            for m in range(max(first, 1), last):
+                if m == 2:
+                    deal_w4(1)
                 for c in range(CHUNKS):
-                    make_y(m, c, y_sb, (CHUNKS * m + c + 4) % BANKS)
-                    gate(result[:, m - first, :], m, y_sb, c, c + 1)
+                    make_out(m, c, result[:, m - first, :], (CHUNKS * m + c + 4) % BANKS)
             nc.sync.dma_start(
-                out=out_rows[first // PACK, :, S * (max(first, 2) % PACK) : S * (first % PACK + last - first)],
-                in_=result[:, max(first, 2) - first :, :].rearrange("p m s -> p (m s)"),
+                out=out_rows[first // PACK, :, S * (first % PACK) : S * (first % PACK + last - first)],
+                in_=result[:].rearrange("p m s -> p (m s)"),
             )

@@ -18,7 +18,6 @@ MULT = mybir.AluOpType.mult
 P = 128
 PACK = 4
 PASSES = K // (P * PACK)
-SCALE_ROWS = 16
 CHUNK = 512
 CHUNKS = S // CHUNK
 H_COLS = 128
@@ -28,25 +27,26 @@ BANK = 2048
 BANKS = 8
 UP_PARTS = 4
 UP_COLS = M // UP_PARTS
-ROW_BYTES = S + M
-SPREAD_FIRST = 48
-SPREAD_STEP = 1
 
 SLOT = 16
-RESULTS_AT = SLOT * M_TILES
 TILE_KIB = 6
+GATES_AT = 8
+RESULTS_AT = GATES_AT + SLOT * M_TILES
+W4_PLANE_AT = RESULTS_AT + TILE_KIB * M_TILES
 STORE_GROUPS = ((0, 4), (4, 7), (7, 8))
-TABLE_AT = (2 * SLOT, 0, SLOT)
-WINDOW_AT = SLOT - 2
-DOWN_RAW_AT = RESULTS_AT
-DOWN_GROUPED_AT = (RESULTS_AT + 24, RESULTS_AT + 28, 4 * SLOT + 8)
-W4_RAW_AT = DOWN_GROUPED_AT[1]
-UP_RAW_AT = DOWN_GROUPED_AT[2]
-PICKED_AT = RESULTS_AT + 36
-STAGE_AT = RESULTS_AT + 40
-DOWN_CODES_AT = 3 * SLOT + 4
-H_GROUPED_AT = (2 * SLOT, 3 * SLOT, 7 * SLOT - 2)
-UP_GROUPED_AT = (6 * SLOT + 4,) + (7 * SLOT - 1,) * (UP_PARTS - 1)
+TABLE_AT = (GATES_AT + 2 * SLOT, GATES_AT + 4 * SLOT)
+DOWN_FIRST_AT = TABLE_AT[0]
+DOWN_REST_AT = RESULTS_AT
+WINDOW_AT = RESULTS_AT + 16
+UP_RAW_AT = W4_PLANE_AT - 16
+W4_RAW_AT = GATES_AT + 7 * SLOT + 4
+W4_ROWS_AT = GATES_AT + SLOT - 2
+DOWN_GROUPED_AT = (TABLE_AT[1], W4_RAW_AT, W4_PLANE_AT - 2)
+PICKED_AT = 0
+LAST_CODES_AT = 0
+DOWN_CODES_AT = (GATES_AT + 7 * SLOT + 12, WINDOW_AT + 8, WINDOW_AT + 10)
+H_GROUPED_AT = tuple(GATES_AT + SLOT * m for m in (5, 6, 7))
+UP_GROUPED_AT = (H_GROUPED_AT[1] + 8,) + (H_GROUPED_AT[2],) * (UP_PARTS - 1)
 
 
 def tile_list_tabgate_none_kernel(
@@ -56,53 +56,43 @@ def tile_list_tabgate_none_kernel(
     with ExitStack() as ctx:
         keep = ctx.enter_context(tc.tile_pool(name="keep", bufs=1))
         arena = ctx.enter_context(tc.tile_pool(name="arena", bufs=1))
-        ring = ctx.enter_context(tc.tile_pool(name="ring", bufs=6))
+        ring = ctx.enter_context(tc.tile_pool(name="ring", bufs=4))
         psum = ctx.enter_context(tc.psum_pool(name="psum", bufs=1))
 
         def placed(shape, dtype, name, kib, align=64):
             return arena.tile(shape, dtype, name=name, offset=1024 * kib, align_bytes=align)
 
         down_rows = down.rearrange("(a p j) r -> p a j r", p=P, j=PACK)
-        down_first = placed([P, PACK, R], F32, "down_first", DOWN_RAW_AT, 4096)
+        down_first = placed([P, PACK, R], F32, "down_first", DOWN_FIRST_AT, 4096)
         nc.sync.dma_start(out=down_first[:], in_=down_rows[:, 0, :, :])
         offsets = keep.tile([P, S // 16], U16, name="offsets")
         nc.sync.dma_start(offsets[:], offs)
 
-        spread = slice(SPREAD_FIRST, SPREAD_FIRST + SPREAD_STEP * PASSES * SCALE_ROWS, SPREAD_STEP)
-        window = placed([P, T // 4], I32, "window", WINDOW_AT)
-        nc.vector.memset(window[0 : spread.start, :], 0)
-        nc.vector.memset(window[spread.stop : P, :], 0)
-        nc.sync.dma_start(out=window[spread, :], in_=tab_scales.bitcast(I32).rearrange("a q t -> (a q) t"))
-        stage = placed([P, ROW_BYTES // 4], I32, "stage", STAGE_AT)
-        nc.sync.dma_start(out=stage[spread, S // 4 :], in_=w4_scales.bitcast(I32).rearrange("a q n -> (a q) n"))
-        down_rest = placed([P, PASSES - 1, PACK, R], F32, "down_rest", DOWN_RAW_AT + 8)
+        window = placed([P, PASSES, T // 4], I32, "window", WINDOW_AT)
+        nc.vector.memset(window[:], 0)
+        nc.scalar.dma_start(out=window[32:96:4, :, :], in_=tab_scales.bitcast(I32).rearrange("a q t -> q a t"))
+        w4_rows = placed([P, PASSES, M], U8, "w4_rows", W4_ROWS_AT)
+        nc.vector.memset(w4_rows[:].bitcast(I32), 0)
+        w4_scale_rows = w4_scales.bitcast(I32).rearrange("a (g r) n -> r g a n", r=4)
+        for r in range(4):
+            nc.sync.dma_start(out=w4_rows[r:P:32, :, :].bitcast(I32), in_=w4_scale_rows[r])
+
+        down_rest = placed([P, PASSES - 1, PACK, R], F32, "down_rest", DOWN_REST_AT)
         nc.sync.dma_start(out=down_rest[:], in_=down_rows[:, 1:PASSES, :, :])
         down_raw = [down_first[:], down_rest[:, 0, :, :], down_rest[:, 1, :, :]]
-        planes = keep.tile([P, PASSES, ROW_BYTES // 4], I32, name="planes", align_bytes=64)
-        nc.vector.memset(planes[:], 0)
+        planes = keep.tile([P, PASSES, S], U8, name="planes", align_bytes=64)
+        nc.vector.memset(planes[:].bitcast(I32), 0)
 
-        picked = placed([P, S], U8, "picked", PICKED_AT)
-        nc.vector.tensor_copy(picked[:], window[:].bitcast(U8).indirect(offsets[:]))
-        nc.vector.tensor_copy(out=stage[:, 0 : S // 4], in_=picked[:].bitcast(I32))
-
-        table = []
+        picked = placed([P, PASSES * S], U8, "picked", PICKED_AT)
         for a in range(PASSES):
-            words = placed([P, T], I32, "words%d" % a, TABLE_AT[a])
-            nc.sync.dma_start(out=words[:], in_=tab_words[a].rearrange("p t i -> p (t i)").bitcast(I32))
-            table.append(words)
-            for r in range(4):
-                first = SPREAD_FIRST + SPREAD_STEP * (SCALE_ROWS * a + r)
-                nc.sync.dma_start(
-                    out=planes[r:P:32, a, :], in_=stage[first : first + 16 * SPREAD_STEP : 4 * SPREAD_STEP, :]
-                )
-        plane_bytes = planes[:].bitcast(U8)
+            nc.vector.tensor_copy(picked[:, S * a : S * (a + 1)], window[:, a, :].bitcast(U8).indirect(offsets[:]))
 
-        down_codes = placed([P, PASSES, R], U32, "down_codes", DOWN_CODES_AT)
-        down_plane = placed([P, PASSES, R], U8, "down_plane", DOWN_CODES_AT + 6)
+        down_codes = [placed([P, R], U32, "down_codes%d" % a, DOWN_CODES_AT[a]) for a in range(PASSES)]
+        down_plane = keep.tile([P, PASSES, R], U8, name="down_plane", align_bytes=64)
         down_grouped = []
         for a in range(PASSES):
             grouped = placed([P, R * PACK], BF16, "down_grouped%d" % a, DOWN_GROUPED_AT[a])
-            interleave = nc.vector.tensor_copy if a == 1 else nc.scalar.copy
+            interleave = nc.vector.tensor_copy if a == 0 else nc.scalar.copy
             interleave(
                 out=grouped[:].rearrange("p (t m j) -> p m j t", t=PACK, j=PACK),
                 in_=down_raw[a].rearrange("p j (m t) -> p m j t", t=PACK),
@@ -110,7 +100,20 @@ def tile_list_tabgate_none_kernel(
             down_grouped.append(grouped)
         for a in range(PASSES):
             nc.vector.quantize_mx(
-                out=down_codes[:, a, :].bitcast(FP8X4), scales=down_plane[:, a, :], in_=down_grouped[a][:]
+                out=down_codes[a][:, :].bitcast(FP8X4), scales=down_plane[:, a, :], in_=down_grouped[a][:]
+            )
+
+        table_rows = tab_words.rearrange("a p t i -> p a (t i)").bitcast(I32)
+        words_first = placed([P, PASSES - 1, T], I32, "words_first", TABLE_AT[0])
+        nc.sync.dma_start(out=words_first[:], in_=table_rows[:, 0 : PASSES - 1, :])
+        words_last = placed([P, T], I32, "words_last", TABLE_AT[1])
+        nc.sync.dma_start(out=words_last[:], in_=table_rows[:, PASSES - 1, :])
+        table = [words_first[:, 0, :], words_first[:, 1, :], words_last[:]]
+
+        for r in range(4):
+            nc.sync.dma_start(
+                out=planes[r:P:32, :, :].rearrange("q a s -> q (a s)").bitcast(I32),
+                in_=picked[32 + 4 * r : 96 : 16, :].bitcast(I32),
             )
 
         w4_raw = placed([P, PASSES, 2 * M], U8, "w4_raw", W4_RAW_AT)
@@ -118,23 +121,24 @@ def tile_list_tabgate_none_kernel(
         up_raw = placed([P, PACK, M], F32, "up_raw", UP_RAW_AT)
         nc.sync.dma_start(out=up_raw[:], in_=up.rearrange("(p j) n -> p j n", j=PACK))
 
-        v_codes = keep.tile([P, PASSES, S], U32, name="v_codes", align_bytes=64)
-        for a in range(PASSES):
-            for c in range(CHUNKS):
+        v_codes = [keep.tile([P, PASSES, CHUNK], U32, name="v_codes%d" % c, align_bytes=64) for c in range(2)]
+        v_codes.append(placed([P, PASSES, CHUNK], U32, "v_codes2", LAST_CODES_AT))
+        for c in range(CHUNKS):
+            for a in range(PASSES):
                 nc.vector.tensor_copy(
-                    v_codes[:, a, CHUNK * c : CHUNK * (c + 1)],
-                    table[a][:].bitcast(U32).indirect(offsets[:, LIST_COLS * c : LIST_COLS * (c + 1)]),
+                    v_codes[c][:, a, :],
+                    table[a].bitcast(U32).indirect(offsets[:, LIST_COLS * c : LIST_COLS * (c + 1)]),
                 )
 
+        w4_plane = placed([P, PASSES, M], U8, "w4_plane", W4_PLANE_AT)
+        nc.vector.tensor_copy(
+            out=w4_plane[:].rearrange("p a (g e q) -> p (a g) e q", e=PACK, q=P),
+            in_=w4_rows[:].rearrange("p a (g q e) -> p (a g) e q", e=PACK, q=P),
+        )
         w4_codes = keep.tile([P, PASSES, 2 * M], U8, name="w4_codes", align_bytes=64)
-        w4_plane = keep.tile([P, PASSES, M], U8, name="w4_plane", align_bytes=64)
 
         def deal_w4(half):
             cols = slice(512 * half, 512 * (half + 1))
-            nc.vector.tensor_copy(
-                out=w4_plane[:, :, cols].rearrange("p a (e q) -> p a e q", e=PACK),
-                in_=plane_bytes[:, :, S + 512 * half : S + 512 * (half + 1)].rearrange("p a (q e) -> p a e q", e=PACK),
-            )
             nc.vector.tensor_copy(
                 out=w4_codes[:].bitcast(U16)[:, :, cols].rearrange("p a (e q) -> p a e q", e=PACK),
                 in_=w4_raw[:].bitcast(U16)[:, :, cols].rearrange("p a (q e) -> p a e q", e=PACK),
@@ -165,10 +169,10 @@ def tile_list_tabgate_none_kernel(
                 for t in range(PACK):
                     nc.tensor.matmul_mx(
                         out=sums[b][:, t, :],
-                        lhsT=down_codes[:, a, P * t : P * (t + 1)].bitcast(FP8X4),
+                        lhsT=down_codes[a][:, P * t : P * (t + 1)].bitcast(FP8X4),
                         lhsT_scale=down_plane[:, a, P * t : P * (t + 1)],
-                        rhs=v_codes[:, a, first : first + H_COLS].bitcast(FP8X4),
-                        rhs_scale=plane_bytes[:, a, first : first + H_COLS],
+                        rhs=v_codes[c][:, a, H_COLS * b : H_COLS * (b + 1)].bitcast(FP8X4),
+                        rhs_scale=planes[:, a, first : first + H_COLS],
                         start=(a == 0 and t == 0),
                         stop=(a == PASSES - 1 and t == PACK - 1),
                     )
@@ -187,7 +191,7 @@ def tile_list_tabgate_none_kernel(
         gate_dealt = gT.rearrange("(g p e) t -> g e p t", p=P, e=PACK)
 
         def load_gates(m):
-            gate_rows = placed([P, T], F32, "gates%d" % m, SLOT * m)
+            gate_rows = placed([P, T], F32, "gates%d" % m, GATES_AT + SLOT * m)
             nc.sync.dma_start(out=gate_rows[:], in_=gate_dealt[m // PACK, m % PACK])
             gates.append(gate_rows)
 
@@ -199,8 +203,8 @@ def tile_list_tabgate_none_kernel(
                     out=acc[:],
                     lhsT=w4_codes[:, a, 2 * P * m : 2 * P * (m + 1)].bitcast(FP4X4),
                     lhsT_scale=w4_plane[:, a, P * m : P * (m + 1)],
-                    rhs=v_codes[:, a, cols].bitcast(FP8X4),
-                    rhs_scale=plane_bytes[:, a, cols],
+                    rhs=v_codes[c][:, a, :].bitcast(FP8X4),
+                    rhs_scale=planes[:, a, cols],
                     start=(a == 0),
                     stop=False,
                 )
@@ -223,14 +227,14 @@ def tile_list_tabgate_none_kernel(
         for a in range(PASSES):
             for c in range(2):
                 h_pass(c, a, first_sums[c])
-        finish_h(0, first_sums[0])
         deal_w4(0)
+        finish_h(0, first_sums[0])
         finish_h(1, first_sums[1])
         last_sums = h_banks((0, 1, 2, 3))
         for a in range(PASSES):
             h_pass(2, a, last_sums)
         make_up(0)
-        for m in range(4):
+        for m in range(M_TILES - 1):
             load_gates(m)
         results = [
             placed([P, last - first, S], F32, "result%d" % first, RESULTS_AT + TILE_KIB * first)
@@ -242,8 +246,7 @@ def tile_list_tabgate_none_kernel(
         make_out(0, 2, results[0][:, 0, :], 6)
         for part in range(1, UP_PARTS):
             make_up(part)
-        for m in range(4, M_TILES):
-            load_gates(m)
+        load_gates(M_TILES - 1)
 
         out_rows = out.rearrange("(g p e) s -> g p (e s)", p=P, e=PACK)
         for (first, last), result in zip(STORE_GROUPS, results):

@@ -255,7 +255,8 @@ def tile_list_tabgate_none_kernel(
                     deal_w4(1)
                 for c in range(CHUNKS):
                     make_out(m, c, result[:, m - first, :], (CHUNKS * m + c + 4) % BANKS)
-            nc.sync.dma_start(
+            queue = nc.scalar if first == PACK else nc.sync
+            queue.dma_start(
                 out=out_rows[first // PACK, :, S * (first % PACK) : S * (first % PACK + last - first)],
                 in_=result[:].rearrange("p m s -> p (m s)"),
             )

from contextlib import ExitStack

import concourse.mybir as mybir

K, M, T, S, R = 1536, 1024, 4096, 1536, 512
FLOPS = 2 * S * (K * R + K * M + R * M)

F32 = mybir.dt.float32
BF16 = mybir.dt.bfloat16
I32 = mybir.dt.int32
U32 = mybir.dt.uint32
U16 = mybir.dt.uint16
U8 = mybir.dt.uint8
FP8X4 = mybir.dt.float8_e4m3fn_x4
FP4X4 = mybir.dt.float4_e2m1fn_x4
MULT = mybir.AluOpType.mult

P = 128
PACK = 4
PASSES = K // (P * PACK)
CHUNK = 512
CHUNKS = S // CHUNK
H_COLS = 128
M_TILES = M // P
LIST_COLS = CHUNK // 16
BANK = 2048
BANKS = 8
UP_PARTS = 4
UP_COLS = M // UP_PARTS

SLOT = 16
TILE_KIB = 6
GATES_AT = 8
RESULTS_AT = GATES_AT + SLOT * M_TILES
W4_PLANE_AT = RESULTS_AT + TILE_KIB * M_TILES
STORE_GROUPS = ((0, 4), (4, 7), (7, 8))
TABLE_AT = (GATES_AT + 2 * SLOT, GATES_AT + 4 * SLOT)
DOWN_FIRST_AT = TABLE_AT[0]
DOWN_REST_AT = RESULTS_AT
WINDOW_AT = RESULTS_AT + 16
UP_RAW_AT = W4_PLANE_AT - 16
W4_RAW_AT = GATES_AT + 7 * SLOT + 4
W4_ROWS_AT = GATES_AT + SLOT - 2
DOWN_GROUPED_AT = (TABLE_AT[1], W4_RAW_AT, W4_PLANE_AT - 2)
PICKED_AT = 0
LAST_CODES_AT = 0
DOWN_CODES_AT = (GATES_AT + 7 * SLOT + 12, WINDOW_AT + 8, WINDOW_AT + 10)
H_GROUPED_AT = tuple(GATES_AT + SLOT * m for m in (5, 6, 7))
UP_GROUPED_AT = (H_GROUPED_AT[1] + 8,) + (H_GROUPED_AT[2],) * (UP_PARTS - 1)


def tile_list_tabgate_none_kernel(
    tc, tab_words, tab_scales, w4_words, w4_scales, down, up, gT, offs, out
):
    nc = tc.nc
    with ExitStack() as ctx:
        keep = ctx.enter_context(tc.tile_pool(name="keep", bufs=1))
        arena = ctx.enter_context(tc.tile_pool(name="arena", bufs=1))
        ring = ctx.enter_context(tc.tile_pool(name="ring", bufs=4))
        psum = ctx.enter_context(tc.psum_pool(name="psum", bufs=1))

        def placed(shape, dtype, name, kib, align=64):
            return arena.tile(shape, dtype, name=name, offset=1024 * kib, align_bytes=align)

        down_rows = down.rearrange("(a p j) r -> p a j r", p=P, j=PACK)
        down_first = placed([P, PACK, R], F32, "down_first", DOWN_FIRST_AT, 4096)
        nc.sync.dma_start(out=down_first[:], in_=down_rows[:, 0, :, :])
        offsets = keep.tile([P, S // 16], U16, name="offsets")
        nc.sync.dma_start(offsets[:], offs)

        window = placed([P, PASSES, T // 4], I32, "window", WINDOW_AT)
        nc.vector.memset(window[:], 0)
        nc.scalar.dma_start(out=window[32:96:4, :, :], in_=tab_scales.bitcast(I32).rearrange("a q t -> q a t"))
        w4_rows = placed([P, PASSES, M], U8, "w4_rows", W4_ROWS_AT)
        nc.vector.memset(w4_rows[:].bitcast(I32), 0)
        w4_scale_rows = w4_scales.bitcast(I32).rearrange("a (g r) n -> r g a n", r=4)
        for r in range(4):
            nc.sync.dma_start(out=w4_rows[r:P:32, :, :].bitcast(I32), in_=w4_scale_rows[r])

        down_rest = placed([P, PASSES - 1, PACK, R], F32, "down_rest", DOWN_REST_AT)
        nc.sync.dma_start(out=down_rest[:], in_=down_rows[:, 1:PASSES, :, :])
        down_raw = [down_first[:], down_rest[:, 0, :, :], down_rest[:, 1, :, :]]
        planes = keep.tile([P, PASSES, S], U8, name="planes", align_bytes=64)
        nc.vector.memset(planes[:].bitcast(I32), 0)

        picked = placed([P, PASSES * S], U8, "picked", PICKED_AT)
        for a in range(PASSES):
            nc.vector.tensor_copy(picked[:, S * a : S * (a + 1)], window[:, a, :].bitcast(U8).indirect(offsets[:]))

        down_codes = [placed([P, R], U32, "down_codes%d" % a, DOWN_CODES_AT[a]) for a in range(PASSES)]
        down_plane = keep.tile([P, PASSES, R], U8, name="down_plane", align_bytes=64)
        down_grouped = []
        for a in range(PASSES):
            grouped = placed([P, R * PACK], BF16, "down_grouped%d" % a, DOWN_GROUPED_AT[a])
            interleave = nc.vector.tensor_copy if a == 0 else nc.scalar.copy
            interleave(
                out=grouped[:].rearrange("p (t m j) -> p m j t", t=PACK, j=PACK),
                in_=down_raw[a].rearrange("p j (m t) -> p m j t", t=PACK),
            )
            down_grouped.append(grouped)
        for a in range(PASSES):
            nc.vector.quantize_mx(
                out=down_codes[a][:, :].bitcast(FP8X4), scales=down_plane[:, a, :], in_=down_grouped[a][:]
            )

        table_rows = tab_words.rearrange("a p t i -> p a (t i)").bitcast(I32)
        words_first = placed([P, PASSES - 1, T], I32, "words_first", TABLE_AT[0])
        nc.sync.dma_start(out=words_first[:], in_=table_rows[:, 0 : PASSES - 1, :])
        words_last = placed([P, T], I32, "words_last", TABLE_AT[1])
        nc.sync.dma_start(out=words_last[:], in_=table_rows[:, PASSES - 1, :])
        table = [words_first[:, 0, :], words_first[:, 1, :], words_last[:]]

        for r in range(4):
            nc.sync.dma_start(
                out=planes[r:P:32, :, :].rearrange("q a s -> q (a s)").bitcast(I32),
                in_=picked[32 + 4 * r : 96 : 16, :].bitcast(I32),
            )

        w4_raw = placed([P, PASSES, 2 * M], U8, "w4_raw", W4_RAW_AT)
        nc.sync.dma_start(out=w4_raw[:].bitcast(I32), in_=w4_words.bitcast(I32).rearrange("a p b -> p a b"))
        up_raw = placed([P, PACK, M], F32, "up_raw", UP_RAW_AT)
        nc.sync.dma_start(out=up_raw[:], in_=up.rearrange("(p j) n -> p j n", j=PACK))

        v_codes = [keep.tile([P, PASSES, CHUNK], U32, name="v_codes%d" % c, align_bytes=64) for c in range(2)]
        v_codes.append(placed([P, PASSES, CHUNK], U32, "v_codes2", LAST_CODES_AT))
        for c in range(CHUNKS):
            for a in range(PASSES):
                nc.vector.tensor_copy(
                    v_codes[c][:, a, :],
                    table[a].bitcast(U32).indirect(offsets[:, LIST_COLS * c : LIST_COLS * (c + 1)]),
                )

        w4_plane = placed([P, PASSES, M], U8, "w4_plane", W4_PLANE_AT)
        nc.vector.tensor_copy(
            out=w4_plane[:].rearrange("p a (g e q) -> p (a g) e q", e=PACK, q=P),
            in_=w4_rows[:].rearrange("p a (g q e) -> p (a g) e q", e=PACK, q=P),
        )
        w4_codes = keep.tile([P, PASSES, 2 * M], U8, name="w4_codes", align_bytes=64)

        def deal_w4(half):
            cols = slice(512 * half, 512 * (half + 1))
            nc.vector.tensor_copy(
                out=w4_codes[:].bitcast(U16)[:, :, cols].rearrange("p a (e q) -> p a e q", e=PACK),
                in_=w4_raw[:].bitcast(U16)[:, :, cols].rearrange("p a (q e) -> p a e q", e=PACK),
            )

        up_codes = keep.tile([P, M], U32, name="up_codes", align_bytes=64)
        up_plane = keep.tile([P, M], U8, name="up_plane", align_bytes=64)
        up_dealt = up_raw[:].rearrange("p j (g q u e) -> p g u q j e", g=2, u=2, e=2)

        def make_up(part):
            cols = slice(UP_COLS * part, UP_COLS * (part + 1))
            grouped = placed([P, UP_COLS * PACK], BF16, "up_grouped%d" % part, UP_GROUPED_AT[part])
            nc.scalar.copy(
                out=grouped[:].rearrange("p (e q j) -> p q j e", e=2, j=PACK),
                in_=up_dealt[:, part // 2, part % 2],
            )
            nc.vector.quantize_mx(out=up_codes[:, cols].bitcast(FP8X4), scales=up_plane[:, cols], in_=grouped[:])

        h_codes = keep.tile([P, S], U32, name="h_codes", align_bytes=64)
        h_plane = keep.tile([P, S], U8, name="h_plane", align_bytes=64)

        def h_banks(banks):
            return [psum.tile([P, PACK, H_COLS], F32, name="h_bank", offset=BANK * b) for b in banks]

        def h_pass(c, a, sums):
            for b in range(CHUNK // H_COLS):
                first = CHUNK * c + H_COLS * b
                for t in range(PACK):
                    nc.tensor.matmul_mx(
                        out=sums[b][:, t, :],
                        lhsT=down_codes[a][:, P * t : P * (t + 1)].bitcast(FP8X4),
                        lhsT_scale=down_plane[:, a, P * t : P * (t + 1)],
                        rhs=v_codes[c][:, a, H_COLS * b : H_COLS * (b + 1)].bitcast(FP8X4),
                        rhs_scale=planes[:, a, first : first + H_COLS],
                        start=(a == 0 and t == 0),
                        stop=(a == PASSES - 1 and t == PACK - 1),
                    )

        def finish_h(c, sums):
            grouped = placed([P, CHUNK * PACK], BF16, "h_grouped%d" % c, H_GROUPED_AT[c])
            for b in range(CHUNK // H_COLS):
                nc.scalar.copy(
                    out=grouped[:, H_COLS * PACK * b : H_COLS * PACK * (b + 1)].rearrange("p (n t) -> p n t", t=PACK),
                    in_=sums[b][:].rearrange("p t n -> p n t"),
                )
            cols = slice(CHUNK * c, CHUNK * (c + 1))
            nc.vector.quantize_mx(out=h_codes[:, cols].bitcast(FP8X4), scales=h_plane[:, cols], in_=grouped[:])

        gates = []
        gate_dealt = gT.rearrange("(g p e) t -> g e p t", p=P, e=PACK)

        def load_gates(m):
            gate_rows = placed([P, T], F32, "gates%d" % m, GATES_AT + SLOT * m)
            nc.sync.dma_start(out=gate_rows[:], in_=gate_dealt[m // PACK, m % PACK])
            gates.append(gate_rows)

        def make_out(m, c, result, bank):
            cols = slice(CHUNK * c, CHUNK * (c + 1))
            acc = psum.tile([P, CHUNK], F32, name="y_bank", offset=BANK * bank)
            for a in range(PASSES):
                nc.tensor.matmul_mx(
                    out=acc[:],
                    lhsT=w4_codes[:, a, 2 * P * m : 2 * P * (m + 1)].bitcast(FP4X4),
                    lhsT_scale=w4_plane[:, a, P * m : P * (m + 1)],
                    rhs=v_codes[c][:, a, :].bitcast(FP8X4),
                    rhs_scale=planes[:, a, cols],
                    start=(a == 0),
                    stop=False,
                )
            nc.tensor.matmul_mx(
                out=acc[:],
                lhsT=up_codes[:, P * m : P * (m + 1)].bitcast(FP8X4),
                lhsT_scale=up_plane[:, P * m : P * (m + 1)],
                rhs=h_codes[:, cols].bitcast(FP8X4),
                rhs_scale=h_plane[:, cols],
                start=False,
                stop=True,
            )
            y_sb = ring.tile([P, CHUNK], F32, name="y_sb")
            nc.scalar.copy(out=y_sb[:], in_=acc[:])
            nc.vector.tensor_tensor(
                result[:, cols], gates[m][:].indirect(offsets[:, LIST_COLS * c : LIST_COLS * (c + 1)]), y_sb[:], MULT
            )

        first_sums = [h_banks((0, 1, 2, 3)), h_banks((4, 5, 6, 7))]
        for a in range(PASSES):
            for c in range(2):
                h_pass(c, a, first_sums[c])
        deal_w4(0)
        finish_h(0, first_sums[0])
        finish_h(1, first_sums[1])
        last_sums = h_banks((0, 1, 2, 3))
        for a in range(PASSES):
            h_pass(2, a, last_sums)
        make_up(0)
        for m in range(M_TILES - 1):
            load_gates(m)
        results = [
            placed([P, last - first, S], F32, "result%d" % first, RESULTS_AT + TILE_KIB * first)
            for first, last in STORE_GROUPS
        ]
        for c in range(2):
            make_out(0, c, results[0][:, 0, :], 4 + c)
        finish_h(2, last_sums)
        make_out(0, 2, results[0][:, 0, :], 6)
        for part in range(1, UP_PARTS):
            make_up(part)
        load_gates(M_TILES - 1)

        out_rows = out.rearrange("(g p e) s -> g p (e s)", p=P, e=PACK)
        for (first, last), result in zip(STORE_GROUPS, results):
            for m in range(max(first, 1), last):
                if m == 2:
                    deal_w4(1)
                for c in range(CHUNKS):
                    make_out(m, c, result[:, m - first, :], (CHUNKS * m + c + 4) % BANKS)
            queue = nc.scalar if first == PACK else nc.sync
            queue.dma_start(
                out=out_rows[first // PACK, :, S * (first % PACK) : S * (first % PACK + last - first)],
                in_=result[:].rearrange("p m s -> p (m s)"),
            )
